import numpy as np
import ml_dtypes


def mxq(x, axis, fmt="e4m3"):
    dtype, down = {"e4m3": (ml_dtypes.float8_e4m3fn, 7), "e5m2": (ml_dtypes.float8_e5m2, 14)}[fmt]
    v = np.moveaxis(np.asarray(x, np.float32).astype(ml_dtypes.bfloat16).astype(np.float64), axis, -1)
    blocks = v.reshape(v.shape[:-1] + (-1, 32))
    amax = np.abs(blocks).max(-1, keepdims=True)
    byte = np.maximum(np.where(amax > 0, np.frexp(amax)[1] - 1 + 127, 0) - down, 1)
    scale = np.exp2(byte - 127.0)
    codes = (blocks / scale).astype(np.float32).astype(dtype).astype(np.float64)
    return np.moveaxis((codes * scale).reshape(v.shape), -1, axis)


WIDE = False


def mx_kscale(k):
    if not WIDE:
        return np.ones(k)
    levels = np.array([10, -10, 5, -5, 0])
    if k % 512:
        return np.exp2(np.random.permutation(np.resize(levels, k // 32))).repeat(32)
    a = np.empty((k // 512, 16))
    for p in range(k // 512):
        a[p, :8] = np.random.permutation(np.resize(levels, 8))
        for g in range(8):
            far = levels[np.abs(levels - a[p, g]) >= 10]
            a[p, g + 8] = far[np.random.randint(len(far))]
    return np.exp2(a.ravel()).repeat(32)


def f64(x):
    return np.asarray(x).astype(np.float64)


def striped(idx):
    return np.tile(idx.reshape(-1, 16).T, (8, 1)).astype(np.uint16)


def unstriped(offs):
    return offs[:16].T.reshape(-1).astype(np.int64)


def pack_weight(w):
    k, n = w.shape
    w = f64(np.asarray(w, np.float32).astype(ml_dtypes.bfloat16)).reshape(k // 32, 32, n)
    amax = np.abs(w).max(1)
    byte = np.clip(np.where(amax > 0, np.frexp(amax)[1] - 1 + 127 - 7, 1), 1, 254)
    scaled = (w * np.exp2(127.0 - byte)[:, None, :]).reshape(k, n).astype(np.float32)
    words = np.ascontiguousarray(scaled.reshape(k // 512, 128, 4, n).transpose(0, 1, 3, 2)).astype(ml_dtypes.float8_e4m3fn).view(np.uint8)
    return words, np.ascontiguousarray(byte.astype(np.uint8).reshape(k // 512, 16, n))


def unpack_weight(words, scales):
    g, p, n, _ = words.shape
    vals = np.ascontiguousarray(words).view(ml_dtypes.float8_e4m3fn).astype(np.float64) * np.repeat(np.exp2(scales.astype(np.float64) - 127.0), 8, axis=1)[..., None]
    return vals.transpose(0, 1, 3, 2).reshape(g * 512, n)


def relu(v):
    return np.maximum(v, 0.0)


K, T, S, V, H, N = 1024, 2048, 1024, 512, 512, 128


def setup_inputs():
    n = np.random.standard_normal
    s = mx_kscale(K)[:, None]
    u = mx_kscale(H)
    packed_xT = pack_weight(n((K, T)) * s)
    packed_w3 = pack_weight(n((H, N)) / np.sqrt(H) / u[:, None])
    return {
        "x_words": packed_xT[0],
        "x_scales": packed_xT[1],
        "w1": (n((K, H)) / np.sqrt(2 * K) / s * u).astype(np.float32),
        "w2": (n((K, H)) / np.sqrt(2 * K) / s * u).astype(np.float32),
        "w3_words": packed_w3[0],
        "w3_scales": packed_w3[1],
        "offs": striped(np.random.permutation(T)[:S]),
        "cen": striped(np.random.permutation(S)[:V]),
        "pos1": striped(np.random.permutation(S)[:V]),
        "pos2": striped(np.random.permutation(S)[:V]),
    }


def reference(x_words, x_scales, w1, w2, w3_words, w3_scales, offs, cen, pos1, pos2):
    xq = unpack_weight(x_words, x_scales)[:, unstriped(offs)]
    y = mxq(f64(w1), 0, "e4m3").T @ xq
    yc = y[:, unstriped(cen)]
    e = mxq(f64(w2), 0, "e4m3").T @ xq
    z = np.maximum(relu(yc + e[:, unstriped(pos1)]), relu(yc + e[:, unstriped(pos2)]))
    return unpack_weight(w3_words, w3_scales).T @ mxq(z, 0, "e4m3")

@@ -1,0 +1,169 @@
+from contextlib import ExitStack
+
+import concourse.mybir as mybir
+
+K, T, S, V, H, N = 1024, 2048, 1024, 512, 512, 128
+FLOPS = 2 * (2 * K * H * S + H * N * V)
+
+F32 = mybir.dt.float32
+BF16 = mybir.dt.bfloat16
+I32 = mybir.dt.int32
+U32 = mybir.dt.uint32
+U16 = mybir.dt.uint16
+U8 = mybir.dt.uint8
+FP8X4 = mybir.dt.float8_e4m3fn_x4
+ALU = mybir.AluOpType
+ACT = mybir.ActivationFunctionType
+
+P = 128
+PACK = 4
+PASSES = K // (P * PACK)
+BANK = 512
+V_SLICES = ((0, 256), (256, 384), (384, 512))
+
+
+def tile_picked_edgecv_relu_p_kernel(tc, x_words, x_scales, w1, w2, w3_words, w3_scales, offs, cen, pos1, pos2, out):
+    nc = tc.nc
+    with ExitStack() as ctx:
+        keep = ctx.enter_context(tc.tile_pool(name="keep", bufs=1))
+        psum = ctx.enter_context(tc.psum_pool(name="psum", bufs=1))
+
+        def sb(shape, dtype, name, tag=None, bufs=1):
+            return keep.tile(shape, dtype, name=name, tag=tag or name, bufs=bufs, align_bytes=64)
+
+        def load_list(src, name):
+            tile = keep.tile(list(src.shape), U16, name=name)
+            nc.sync.dma_start(tile[:], src)
+            return tile
+
+        def load_words(z):
+            tile = sb([P, T], I32, "x_table%d" % (z,))
+            nc.sync.dma_start(tile[:], x_words[z].rearrange("p c r -> p (c r)").bitcast(I32))
+            return tile
+
+        def load_weight(w, z, c0, c1, name):
+            tile = sb([P, PACK, c1 - c0], F32, name)
+            nc.sync.dma_start(tile[:], w[z * 512:(z + 1) * 512, c0:c1].rearrange("(p j) c -> p j c", j=PACK))
+            return tile
+
+        def cast_weight(copy, grouped, raw, m0, m1):
+            copy(grouped[:, :, m0:m1, :].rearrange("p t m j -> p m j t"), raw[:].rearrange("p j (m t) -> p m j t", t=PACK))
+
+        def scalar_copy(dst, src):
+            nc.scalar.activation(dst, src, ACT.Copy)
+
+        def quantise(grouped, t0, t1, name):
+            width = (t1 - t0) * P
+            codes = sb([P, width], U32, name + "_codes")
+            scales = sb([P, width], U8, name + "_scales")
+            nc.vector.quantize_mx(out=codes[:].bitcast(FP8X4), scales=scales[:], in_=grouped[:, t0:t1].rearrange("p t m j -> p (t m j)"))
+            return [(codes[:, i * P:(i + 1) * P], scales[:, i * P:(i + 1) * P]) for i in range(t1 - t0)]
+
+        def gather_words(table, z, half):
+            tile = sb([P, BANK], U32, "x_picked%d_%d" % (z, half,))
+            nc.vector.tensor_copy(tile[:], table[:].bitcast(U32).indirect(offs_sb[:, half * 32:(half + 1) * 32]))
+            return tile
+
+        def product(weights, name):
+            rows = sb([P, S], F32, name)
+            for half in range(2):
+                cols = slice(half * BANK, (half + 1) * BANK)
+                acc = psum.tile([P, BANK], F32, name="acc", tag="acc", bufs=6)
+                for z in range(PASSES):
+                    nc.tensor.matmul_mx(
+                        out=acc[:], lhsT=weights[z][0].bitcast(FP8X4), lhsT_scale=weights[z][1],
+                        rhs=picked[z][half][:].bitcast(FP8X4), rhs_scale=picked_scales[4 * z:P, cols],
+                        start=(z == 0), stop=(z == PASSES - 1))
+                nc.scalar.copy(rows[:, cols], acc[:])
+            return rows
+
+        x_scale_table = sb([P, T], U8, "x_scale_table")
+        nc.vector.memset(x_scale_table[:].bitcast(I32), 0)
+        w3_scale = sb([P, N], U8, "w3_scale")
+        nc.vector.memset(w3_scale[:].bitcast(I32), 0)
+
+        table0 = load_words(0)
+        offs_sb = load_list(offs, "offs_sb")
+        raw20 = load_weight(w2, 0, 0, H, "raw20")
+        for q in range(4):
+            nc.sync.dma_start(x_scale_table[32 * q:32 * q + 8, :].bitcast(I32), x_scales[:, 4 * q:4 * q + 4, :].bitcast(I32))
+        table1 = load_words(1)
+        raw21a = load_weight(w2, 1, 0, 256, "raw21a")
+        raw21b = load_weight(w2, 1, 256, H, "raw21b")
+        pos1_sb = load_list(pos1, "pos1_sb")
+        pos2_sb = load_list(pos2, "pos2_sb")
+        raw10 = load_weight(w1, 0, 0, H, "raw10")
+        raw11 = load_weight(w1, 1, 0, H, "raw11")
+        cen_sb = load_list(cen, "cen_sb")
+        w3_code = sb([P, N], U32, "w3_code")
+        nc.sync.dma_start(w3_code[:].bitcast(I32), w3_words[0].rearrange("p c r -> p (c r)").bitcast(I32))
+        for q in range(4):
+            nc.sync.dma_start(w3_scale[32 * q:32 * q + 4, :].bitcast(I32), w3_scales[0, 4 * q:4 * q + 4, :].bitcast(I32))
+
+        picked = [[gather_words(table0, 0, half) for half in range(2)]]
+        picked_scales = sb([P, S], U8, "picked_scales")
+        nc.vector.tensor_copy(picked_scales[:], x_scale_table[:].indirect(offs_sb[:]))
+
+        g20 = sb([P, PACK, P, PACK], BF16, "g20")
+        cast_weight(scalar_copy, g20, raw20, 0, P)
+        q20 = quantise(g20, 0, 4, "w20")
+        picked.append([gather_words(table1, 1, half) for half in range(2)])
+        g21 = sb([P, PACK, P, PACK], BF16, "g21")
+        cast_weight(scalar_copy, g21, raw21a, 0, 64)
+        cast_weight(nc.vector.tensor_copy, g21, raw21b, 64, P)
+        q21 = quantise(g21, 0, 1, "w21a") + quantise(g21, 1, 2, "w21b") + quantise(g21, 2, 4, "w21c")
+
+        def neighbours(e_rows, t, tag):
+            first = sb([P, V], F32, "first%d" % (t,), tag=tag)
+            nc.vector.tensor_copy(first[:], e_rows[:].indirect(pos1_sb[:]))
+            second = sb([P, V], F32, "second%d" % (t,))
+            nc.vector.tensor_copy(second[:], e_rows[:].indirect(pos2_sb[:]))
+            return first, second
+
+        def larger(pair, t):
+            tile = sb([P, V], F32, "larger%d" % (t,))
+            nc.vector.tensor_tensor(tile[:], pair[0][:], pair[1][:], ALU.max)
+            return tile
+
+        def quantise_w1(raw, z):
+            grouped = sb([P, PACK, P, PACK], BF16, "g1%d" % (z,), tag="hold%d" % (z,))
+            cast_weight(scalar_copy, grouped, raw, 0, P)
+            return quantise(grouped, 0, 4, "w1%d" % (z,))
+
+        e0 = product([q20[0], q21[0]], "e0")
+        e1 = product([q20[1], q21[1]], "e1")
+        pair0 = neighbours(e0, 0, None)
+        pair1 = neighbours(e1, 1, None)
+        m = [larger(pair0, 0)]
+        q10 = quantise_w1(raw10, 0)
+        e2 = product([q20[2], q21[2]], "e2")
+        e3 = product([q20[3], q21[3]], "e3")
+        pair2 = neighbours(e2, 2, "hold0")
+        m.append(larger(pair1, 1))
+        q11 = quantise_w1(raw11, 1)
+        y = [product([q10[t], q11[t]], "y%d" % (t,)) for t in range(4)]
+        pair3 = neighbours(e3, 3, "hold1")
+        m.append(larger(pair2, 2))
+        m.append(larger(pair3, 3))
+
+        for i, (v0, v1) in enumerate(V_SLICES):
+            n = v1 - v0
+            edge = sb([P, PACK, n], F32, "edge%d" % (i,))
+            for t in range(4):
+                nc.vector.tensor_tensor(edge[:, t, :], y[t][:].indirect(cen_sb[:, v0 // 16:v1 // 16]), m[t][:, v0:v1], ALU.add)
+            z = sb([P, n, PACK], BF16, "z%d" % (i,))
+            z_view = z[:].rearrange("p (c i) t -> p c t i", i=4)
+            edge_view = edge[:].rearrange("p t (c i) -> p c t i", i=4)
+            if i < len(V_SLICES) - 1:
+                nc.scalar.activation(z_view, edge_view, ACT.Relu)
+            else:
+                nc.vector.tensor_scalar_max(z_view, edge_view, 0.0)
+            z_codes = sb([P, n], U32, "z_codes%d" % (i,))
+            z_scales = sb([P, n], U8, "z_scales%d" % (i,))
+            nc.vector.quantize_mx(out=z_codes[:].bitcast(FP8X4), scales=z_scales[:], in_=z[:].rearrange("p c t -> p (c t)"))
+            res = psum.tile([P, n], F32, name="res", tag="res", bufs=2)
+            nc.tensor.matmul_mx(out=res[:], lhsT=w3_code[:].bitcast(FP8X4), lhsT_scale=w3_scale[:],
+                                rhs=z_codes[:].bitcast(FP8X4), rhs_scale=z_scales[:], start=True, stop=True)
+            res_sb = sb([P, n], F32, "res_sb%d" % (i,))
+            nc.scalar.copy(res_sb[:], res[:])
+            nc.sync.dma_start(out[:, v0:v1], res_sb[:])

@@ -19,7 +19,6 @@ P = 128
 PACK = 4
 PASSES = K // (P * PACK)
 BANK = 512
-V_SLICES = ((0, 256), (256, 384), (384, 512))
 
 
 def tile_picked_edgecv_relu_p_kernel(tc, x_words, x_scales, w1, w2, w3_words, w3_scales, offs, cen, pos1, pos2, out):
@@ -46,35 +45,35 @@ def tile_picked_edgecv_relu_p_kernel(tc, x_words, x_scales, w1, w2, w3_words, w3
             nc.sync.dma_start(tile[:], w[z * 512:(z + 1) * 512, c0:c1].rearrange("(p j) c -> p j c", j=PACK))
             return tile
 
-        def cast_weight(copy, grouped, raw, m0, m1):
-            copy(grouped[:, :, m0:m1, :].rearrange("p t m j -> p m j t"), raw[:].rearrange("p j (m t) -> p m j t", t=PACK))
-
-        def scalar_copy(dst, src):
+        def scalar_cast(dst, src):
             nc.scalar.activation(dst, src, ACT.Copy)
 
-        def quantise(grouped, t0, t1, name):
-            width = (t1 - t0) * P
+        def quantise_weight(raw, name):
+            width = raw.shape[2]
+            grouped = sb([P, PACK, width // PACK, PACK], BF16, name + "_grouped")
+            scalar_cast(grouped[:].rearrange("p t m j -> p m j t"), raw[:].rearrange("p j (m t) -> p m j t", t=PACK))
             codes = sb([P, width], U32, name + "_codes")
             scales = sb([P, width], U8, name + "_scales")
-            nc.vector.quantize_mx(out=codes[:].bitcast(FP8X4), scales=scales[:], in_=grouped[:, t0:t1].rearrange("p t m j -> p (t m j)"))
-            return [(codes[:, i * P:(i + 1) * P], scales[:, i * P:(i + 1) * P]) for i in range(t1 - t0)]
+            nc.vector.quantize_mx(out=codes[:].bitcast(FP8X4), scales=scales[:], in_=grouped[:].rearrange("p t m j -> p (t m j)"))
+            return [(codes[:, i:i + P], scales[:, i:i + P]) for i in range(0, width, P)]
 
-        def gather_words(table, z, half):
-            tile = sb([P, BANK], U32, "x_picked%d_%d" % (z, half,))
-            nc.vector.tensor_copy(tile[:], table[:].bitcast(U32).indirect(offs_sb[:, half * 32:(half + 1) * 32]))
+        def gather_words(table, z, tag=None):
+            tile = sb([P, S], U32, "x_picked%d" % z, tag=tag)
+            for half in range(2):
+                nc.vector.tensor_copy(tile[:, half * BANK:(half + 1) * BANK], table[:].bitcast(U32).indirect(offs_sb[:, half * 32:(half + 1) * 32]))
             return tile
 
-        def product(weights, name):
-            rows = sb([P, S], F32, name)
+        def product(weights, name, second_copy=nc.scalar.copy, tag=None):
+            rows = sb([P, S], F32, name, tag=tag)
             for half in range(2):
                 cols = slice(half * BANK, (half + 1) * BANK)
-                acc = psum.tile([P, BANK], F32, name="acc", tag="acc", bufs=6)
+                acc = psum.tile([P, BANK], F32, name="acc", tag="acc", bufs=8)
                 for z in range(PASSES):
                     nc.tensor.matmul_mx(
                         out=acc[:], lhsT=weights[z][0].bitcast(FP8X4), lhsT_scale=weights[z][1],
-                        rhs=picked[z][half][:].bitcast(FP8X4), rhs_scale=picked_scales[4 * z:P, cols],
+                        rhs=picked[z][:, cols].bitcast(FP8X4), rhs_scale=picked_scales[4 * z:P, cols],
                         start=(z == 0), stop=(z == PASSES - 1))
-                nc.scalar.copy(rows[:, cols], acc[:])
+                (second_copy if half else nc.scalar.copy)(rows[:, cols], acc[:])
             return rows
 
         x_scale_table = sb([P, T], U8, "x_scale_table")
@@ -84,14 +83,15 @@ def tile_picked_edgecv_relu_p_kernel(tc, x_words, x_scales, w1, w2, w3_words, w3
 
         table0 = load_words(0)
         offs_sb = load_list(offs, "offs_sb")
-        raw20 = load_weight(w2, 0, 0, H, "raw20")
         for q in range(4):
             nc.sync.dma_start(x_scale_table[32 * q:32 * q + 8, :].bitcast(I32), x_scales[:, 4 * q:4 * q + 4, :].bitcast(I32))
+        raw200 = load_weight(w2, 0, 0, 256, "raw200")
         table1 = load_words(1)
-        raw21a = load_weight(w2, 1, 0, 256, "raw21a")
-        raw21b = load_weight(w2, 1, 256, H, "raw21b")
+        raw201 = load_weight(w2, 1, 0, 256, "raw201")
+        raw210 = load_weight(w2, 0, 256, H, "raw210")
         pos1_sb = load_list(pos1, "pos1_sb")
         pos2_sb = load_list(pos2, "pos2_sb")
+        raw211 = load_weight(w2, 1, 256, H, "raw211")
         raw10 = load_weight(w1, 0, 0, H, "raw10")
         raw11 = load_weight(w1, 1, 0, H, "raw11")
         cen_sb = load_list(cen, "cen_sb")
@@ -100,70 +100,83 @@ def tile_picked_edgecv_relu_p_kernel(tc, x_words, x_scales, w1, w2, w3_words, w3
         for q in range(4):
             nc.sync.dma_start(w3_scale[32 * q:32 * q + 4, :].bitcast(I32), w3_scales[0, 4 * q:4 * q + 4, :].bitcast(I32))
 
-        picked = [[gather_words(table0, 0, half) for half in range(2)]]
+        picked = [gather_words(table0, 0)]
         picked_scales = sb([P, S], U8, "picked_scales")
         nc.vector.tensor_copy(picked_scales[:], x_scale_table[:].indirect(offs_sb[:]))
+        q200 = quantise_weight(raw200, "w200")
+        picked.append(gather_words(table1, 1, "w200_grouped"))
+        q201 = quantise_weight(raw201, "w201")
+        q210 = quantise_weight(raw210, "w210")
 
-        g20 = sb([P, PACK, P, PACK], BF16, "g20")
-        cast_weight(scalar_copy, g20, raw20, 0, P)
-        q20 = quantise(g20, 0, 4, "w20")
-        picked.append([gather_words(table1, 1, half) for half in range(2)])
-        g21 = sb([P, PACK, P, PACK], BF16, "g21")
-        cast_weight(scalar_copy, g21, raw21a, 0, 64)
-        cast_weight(nc.vector.tensor_copy, g21, raw21b, 64, P)
-        q21 = quantise(g21, 0, 1, "w21a") + quantise(g21, 1, 2, "w21b") + quantise(g21, 2, 4, "w21c")
+        edge = [sb([P, PACK, 256], F32, "edge%d" % (i,)) for i in range(2)]
+        m = [sb([P, V], F32, "larger%d" % (t,)) for t in range(3)]
+        m3_second = sb([P, 256], F32, "larger3")
+        m_half = [[m[t][:, 0:256] for t in range(3)] + [edge[1][:, 2, :]], [m[t][:, 256:V] for t in range(3)] + [m3_second[:]]]
 
-        def neighbours(e_rows, t, tag):
-            first = sb([P, V], F32, "first%d" % (t,), tag=tag)
+        def neighbours(e_rows, i):
+            first = sb([P, V], F32, "first%d" % (i,))
             nc.vector.tensor_copy(first[:], e_rows[:].indirect(pos1_sb[:]))
-            second = sb([P, V], F32, "second%d" % (t,))
+            second = sb([P, V], F32, "second%d" % (i,))
             nc.vector.tensor_copy(second[:], e_rows[:].indirect(pos2_sb[:]))
             return first, second
 
-        def larger(pair, t):
-            tile = sb([P, V], F32, "larger%d" % (t,))
+        def larger(pair, hh, s):
+            tile = sb([P, V], F32, "unplaced%d_%d" % (hh, s,))
             nc.vector.tensor_tensor(tile[:], pair[0][:], pair[1][:], ALU.max)
-            return tile
+            for u in range(2):
+                src = tile[64 * u:64 * u + 64, :]
+                rows = slice(64 * hh, 64 * hh + 64)
+                if 2 * s + u < 3:
+                    nc.sync.dma_start(m[2 * s + u][rows, :], src)
+                else:
+                    for i in range(2):
+                        nc.sync.dma_start(m_half[i][3][rows, :], src[:, 256 * i:256 * i + 256])
 
-        def quantise_w1(raw, z):
-            grouped = sb([P, PACK, P, PACK], BF16, "g1%d" % (z,), tag="hold%d" % (z,))
-            cast_weight(scalar_copy, grouped, raw, 0, P)
-            return quantise(grouped, 0, 4, "w1%d" % (z,))
-
-        e0 = product([q20[0], q21[0]], "e0")
-        e1 = product([q20[1], q21[1]], "e1")
-        pair0 = neighbours(e0, 0, None)
-        pair1 = neighbours(e1, 1, None)
-        m = [larger(pair0, 0)]
-        q10 = quantise_w1(raw10, 0)
-        e2 = product([q20[2], q21[2]], "e2")
-        e3 = product([q20[3], q21[3]], "e3")
-        pair2 = neighbours(e2, 2, "hold0")
-        m.append(larger(pair1, 1))
-        q11 = quantise_w1(raw11, 1)
+        e0 = product([q200[0], q201[0]], "e0", nc.vector.tensor_copy)
+        pair0 = neighbours(e0, 0)
+        q211 = quantise_weight(raw211, "w211")
+        e1 = product([q200[1], q201[1]], "e1", tag="raw211")
+        pair1 = neighbours(e1, 1)
+        larger(pair0, 0, 0)
+        q10 = quantise_weight(raw10, "w10")
+        e2 = product([q210[0], q211[0]], "e2", tag="raw10")
+        pair2 = neighbours(e2, 2)
+        larger(pair1, 0, 1)
+        q11 = quantise_weight(raw11, "w11")
+        e3 = product([q210[1], q211[1]], "e3", tag="raw11")
+        pair3 = neighbours(e3, 3)
+        larger(pair2, 1, 0)
+        larger(pair3, 1, 1)
         y = [product([q10[t], q11[t]], "y%d" % (t,)) for t in range(4)]
-        pair3 = neighbours(e3, 3, "hold1")
-        m.append(larger(pair2, 2))
-        m.append(larger(pair3, 3))
 
-        for i, (v0, v1) in enumerate(V_SLICES):
+        def add_centres(i, t):
+            nc.vector.tensor_tensor(edge[i][:, t, :], y[t][:].indirect(cen_sb[:, 16 * i:16 * i + 16]), m_half[i][t], ALU.add)
+
+        def scalar_relu(dst, src):
+            nc.scalar.activation(dst, src, ACT.Relu)
+
+        def vector_relu(dst, src):
+            nc.vector.tensor_scalar_max(dst, src, 0.0)
+
+        def project(v0, v1, relu):
             n = v1 - v0
-            edge = sb([P, PACK, n], F32, "edge%d" % (i,))
-            for t in range(4):
-                nc.vector.tensor_tensor(edge[:, t, :], y[t][:].indirect(cen_sb[:, v0 // 16:v1 // 16]), m[t][:, v0:v1], ALU.add)
-            z = sb([P, n, PACK], BF16, "z%d" % (i,))
-            z_view = z[:].rearrange("p (c i) t -> p c t i", i=4)
-            edge_view = edge[:].rearrange("p t (c i) -> p c t i", i=4)
-            if i < len(V_SLICES) - 1:
-                nc.scalar.activation(z_view, edge_view, ACT.Relu)
-            else:
-                nc.vector.tensor_scalar_max(z_view, edge_view, 0.0)
-            z_codes = sb([P, n], U32, "z_codes%d" % (i,))
-            z_scales = sb([P, n], U8, "z_scales%d" % (i,))
+            z = sb([P, n, PACK], BF16, "z%d" % v0)
+            sums = edge[v0 // 256][:, :, v0 % 256:v0 % 256 + n]
+            relu(z[:].rearrange("p (c i) t -> p c t i", i=4), sums.rearrange("p t (c i) -> p c t i", i=4))
+            z_codes = sb([P, n], U32, "z_codes%d" % v0)
+            z_scales = sb([P, n], U8, "z_scales%d" % v0)
             nc.vector.quantize_mx(out=z_codes[:].bitcast(FP8X4), scales=z_scales[:], in_=z[:].rearrange("p c t -> p (c t)"))
-            res = psum.tile([P, n], F32, name="res", tag="res", bufs=2)
+            res = psum.tile([P, n], F32, name="res", tag="acc", bufs=8)
             nc.tensor.matmul_mx(out=res[:], lhsT=w3_code[:].bitcast(FP8X4), lhsT_scale=w3_scale[:],
                                 rhs=z_codes[:].bitcast(FP8X4), rhs_scale=z_scales[:], start=True, stop=True)
-            res_sb = sb([P, n], F32, "res_sb%d" % (i,))
+            res_sb = sb([P, n], F32, "res_sb%d" % v0)
             nc.scalar.copy(res_sb[:], res[:])
             nc.sync.dma_start(out[:, v0:v1], res_sb[:])
+
+        for t in range(4):
+            add_centres(0, t)
+        for t in range(4):
+            add_centres(1, t)
+        project(0, 256, scalar_relu)
+        project(256, 384, scalar_relu)
+        project(384, 512, vector_relu)

@@ -18,7 +18,8 @@ ACT = mybir.ActivationFunctionType
 P = 128
 PACK = 4
 PASSES = K // (P * PACK)
-BANK = 512
+HALVES = ((0, 512), (512, 1024))
+TAPERED = ((0, 512), (512, 768), (768, 1024))
 
 
 def tile_picked_edgecv_relu_p_kernel(tc, x_words, x_scales, w1, w2, w3_words, w3_scales, offs, cen, pos1, pos2, out):
@@ -48,32 +49,32 @@ def tile_picked_edgecv_relu_p_kernel(tc, x_words, x_scales, w1, w2, w3_words, w3
         def scalar_cast(dst, src):
             nc.scalar.activation(dst, src, ACT.Copy)
 
-        def quantise_weight(raw, name):
-            width = raw.shape[2]
-            grouped = sb([P, PACK, width // PACK, PACK], BF16, name + "_grouped")
-            scalar_cast(grouped[:].rearrange("p t m j -> p m j t"), raw[:].rearrange("p j (m t) -> p m j t", t=PACK))
-            codes = sb([P, width], U32, name + "_codes")
-            scales = sb([P, width], U8, name + "_scales")
-            nc.vector.quantize_mx(out=codes[:].bitcast(FP8X4), scales=scales[:], in_=grouped[:].rearrange("p t m j -> p (t m j)"))
-            return [(codes[:, i:i + P], scales[:, i:i + P]) for i in range(0, width, P)]
+        def quantise_weight(raws, name, codes_tag=None):
+            width = raws[0].shape[2]
+            grouped = sb([P, len(raws), PACK, width // PACK, PACK], BF16, name + "_grouped")
+            for z, raw in enumerate(raws):
+                scalar_cast(grouped[:, z].rearrange("p t m j -> p m j t"), raw[:].rearrange("p j (m t) -> p m j t", t=PACK))
+            codes = sb([P, len(raws) * width], U32, name + "_codes", tag=codes_tag)
+            scales = sb([P, len(raws) * width], U8, name + "_scales")
+            nc.vector.quantize_mx(out=codes[:].bitcast(FP8X4), scales=scales[:], in_=grouped[:].rearrange("p z t m j -> p (z t m j)"))
+            return [(codes[:, i:i + P], scales[:, i:i + P]) for i in range(0, len(raws) * width, P)]
 
-        def gather_words(table, z, tag=None):
+        def gather_words(table, z, pieces, tag=None):
             tile = sb([P, S], U32, "x_picked%d" % z, tag=tag)
-            for half in range(2):
-                nc.vector.tensor_copy(tile[:, half * BANK:(half + 1) * BANK], table[:].bitcast(U32).indirect(offs_sb[:, half * 32:(half + 1) * 32]))
+            for c0, c1 in pieces:
+                nc.vector.tensor_copy(tile[:, c0:c1], table[:].bitcast(U32).indirect(offs_sb[:, c0 // 16:c1 // 16]))
             return tile
 
-        def product(weights, name, second_copy=nc.scalar.copy, tag=None):
+        def product(weights, name, pieces=HALVES, last_copy=nc.scalar.copy, tag=None):
             rows = sb([P, S], F32, name, tag=tag)
-            for half in range(2):
-                cols = slice(half * BANK, (half + 1) * BANK)
-                acc = psum.tile([P, BANK], F32, name="acc", tag="acc", bufs=8)
+            for c0, c1 in pieces:
+                acc = psum.tile([P, c1 - c0], F32, name="acc", tag="acc", bufs=8)
                 for z in range(PASSES):
                     nc.tensor.matmul_mx(
                         out=acc[:], lhsT=weights[z][0].bitcast(FP8X4), lhsT_scale=weights[z][1],
-                        rhs=picked[z][:, cols].bitcast(FP8X4), rhs_scale=picked_scales[4 * z:P, cols],
+                        rhs=picked[z][:, c0:c1].bitcast(FP8X4), rhs_scale=picked_scales[4 * z:P, c0:c1],
                         start=(z == 0), stop=(z == PASSES - 1))
-                (second_copy if half else nc.scalar.copy)(rows[:, cols], acc[:])
+                (last_copy if c1 == S else nc.scalar.copy)(rows[:, c0:c1], acc[:])
             return rows
 
         x_scale_table = sb([P, T], U8, "x_scale_table")
@@ -85,13 +86,12 @@ def tile_picked_edgecv_relu_p_kernel(tc, x_words, x_scales, w1, w2, w3_words, w3
         offs_sb = load_list(offs, "offs_sb")
         for q in range(4):
             nc.sync.dma_start(x_scale_table[32 * q:32 * q + 8, :].bitcast(I32), x_scales[:, 4 * q:4 * q + 4, :].bitcast(I32))
-        raw200 = load_weight(w2, 0, 0, 256, "raw200")
+        raw_a = [load_weight(w2, z, 0, 128, "raw_a%d" % z) for z in range(PASSES)]
         table1 = load_words(1)
-        raw201 = load_weight(w2, 1, 0, 256, "raw201")
-        raw210 = load_weight(w2, 0, 256, H, "raw210")
+        raw_b = [load_weight(w2, z, 128, 256, "raw_b%d" % z) for z in range(PASSES)]
         pos1_sb = load_list(pos1, "pos1_sb")
         pos2_sb = load_list(pos2, "pos2_sb")
-        raw211 = load_weight(w2, 1, 256, H, "raw211")
+        raw_c = [load_weight(w2, z, 256, H, "raw_c%d" % z) for z in range(PASSES)]
         raw10 = load_weight(w1, 0, 0, H, "raw10")
         raw11 = load_weight(w1, 1, 0, H, "raw11")
         cen_sb = load_list(cen, "cen_sb")
@@ -100,13 +100,12 @@ def tile_picked_edgecv_relu_p_kernel(tc, x_words, x_scales, w1, w2, w3_words, w3
         for q in range(4):
             nc.sync.dma_start(w3_scale[32 * q:32 * q + 4, :].bitcast(I32), w3_scales[0, 4 * q:4 * q + 4, :].bitcast(I32))
 
-        picked = [gather_words(table0, 0)]
+        picked = [gather_words(table0, 0, ((0, S),))]
         picked_scales = sb([P, S], U8, "picked_scales")
         nc.vector.tensor_copy(picked_scales[:], x_scale_table[:].indirect(offs_sb[:]))
-        q200 = quantise_weight(raw200, "w200")
-        picked.append(gather_words(table1, 1, "w200_grouped"))
-        q201 = quantise_weight(raw201, "w201")
-        q210 = quantise_weight(raw210, "w210")
+        qa = quantise_weight(raw_a, "wa")
+        picked.append(gather_words(table1, 1, TAPERED, "wa_grouped"))
+        qb = quantise_weight(raw_b, "wb", "x_table1")
 
         edge = [sb([P, PACK, 256], F32, "edge%d" % (i,)) for i in range(2)]
         m = [sb([P, V], F32, "larger%d" % (t,)) for t in range(3)]
@@ -117,36 +116,36 @@ def tile_picked_edgecv_relu_p_kernel(tc, x_words, x_scales, w1, w2, w3_words, w3
             first = sb([P, V], F32, "first%d" % (i,))
             nc.vector.tensor_copy(first[:], e_rows[:].indirect(pos1_sb[:]))
             second = sb([P, V], F32, "second%d" % (i,))
-            nc.vector.tensor_copy(second[:], e_rows[:].indirect(pos2_sb[:]))
+            for i in range(2):
+                nc.vector.tensor_copy(second[:, 256 * i:256 * i + 256], e_rows[:].indirect(pos2_sb[:, 16 * i:16 * i + 16]))
             return first, second
 
-        def larger(pair, hh, s):
-            tile = sb([P, V], F32, "unplaced%d_%d" % (hh, s,))
-            nc.vector.tensor_tensor(tile[:], pair[0][:], pair[1][:], ALU.max)
-            for u in range(2):
-                src = tile[64 * u:64 * u + 64, :]
-                rows = slice(64 * hh, 64 * hh + 64)
-                if 2 * s + u < 3:
-                    nc.sync.dma_start(m[2 * s + u][rows, :], src)
+        def larger(pair, c0, width, t0):
+            tile = sb([P, V], F32, "unplaced%d_%d" % (c0, t0))
+            for i in range(2):
+                cols = slice(256 * i, 256 * i + 256)
+                nc.vector.tensor_tensor(tile[:, cols], pair[0][:, cols], pair[1][:, cols], ALU.max)
+            run = width // PACK
+            rows = slice(c0 // PACK, c0 // PACK + run)
+            for u in range(P // run):
+                src = tile[run * u:run * u + run, :]
+                if t0 + u < 3:
+                    nc.sync.dma_start(m[t0 + u][rows, :], src)
                 else:
                     for i in range(2):
                         nc.sync.dma_start(m_half[i][3][rows, :], src[:, 256 * i:256 * i + 256])
 
-        e0 = product([q200[0], q201[0]], "e0", nc.vector.tensor_copy)
-        pair0 = neighbours(e0, 0)
-        q211 = quantise_weight(raw211, "w211")
-        e1 = product([q200[1], q201[1]], "e1", tag="raw211")
-        pair1 = neighbours(e1, 1)
-        larger(pair0, 0, 0)
-        q10 = quantise_weight(raw10, "w10")
-        e2 = product([q210[0], q211[0]], "e2", tag="raw10")
-        pair2 = neighbours(e2, 2)
-        larger(pair1, 0, 1)
-        q11 = quantise_weight(raw11, "w11")
-        e3 = product([q210[1], q211[1]], "e3", tag="raw11")
-        pair3 = neighbours(e3, 3)
-        larger(pair2, 1, 0)
-        larger(pair3, 1, 1)
+        e0 = product(qa, "e0", TAPERED, nc.vector.tensor_copy)
+        larger(neighbours(e0, 0), 0, 128, 0)
+        qc = quantise_weight(raw_c, "wc")
+        e1 = product(qb, "e1", tag="raw_c0")
+        larger(neighbours(e1, 1), 128, 128, 0)
+        q10 = quantise_weight([raw10], "w10")
+        e2 = product([qc[0], qc[2]], "e2")
+        larger(neighbours(e2, 2), 256, 256, 0)
+        q11 = quantise_weight([raw11], "w11")
+        e3 = product([qc[1], qc[3]], "e3")
+        larger(neighbours(e3, 3), 256, 256, 2)
         y = [product([q10[t], q11[t]], "y%d" % (t,)) for t in range(4)]
 
         def add_centres(i, t):

@@ -108,9 +108,7 @@ def tile_picked_edgecv_relu_p_kernel(tc, x_words, x_scales, w1, w2, w3_words, w3
         qb = quantise_weight(raw_b, "wb", "x_table1")
 
         edge = [sb([P, PACK, 256], F32, "edge%d" % (i,)) for i in range(2)]
-        m = [sb([P, V], F32, "larger%d" % (t,)) for t in range(3)]
-        m3_second = sb([P, 256], F32, "larger3")
-        m_half = [[m[t][:, 0:256] for t in range(3)] + [edge[1][:, 2, :]], [m[t][:, 256:V] for t in range(3)] + [m3_second[:]]]
+        m_half = [[sb([P, 256], F32, "larger%d_%d" % (i, t))[:] if (i, t) != (0, 3) else edge[1][:, 2, :] for t in range(4)] for i in range(2)]
 
         def neighbours(e_rows, i):
             first = sb([P, V], F32, "first%d" % (i,))
@@ -122,18 +120,13 @@ def tile_picked_edgecv_relu_p_kernel(tc, x_words, x_scales, w1, w2, w3_words, w3
 
         def larger(pair, c0, width, t0):
             tile = sb([P, V], F32, "unplaced%d_%d" % (c0, t0))
+            run = width // PACK
+            rows = slice(c0 // PACK, c0 // PACK + run)
             for i in range(2):
                 cols = slice(256 * i, 256 * i + 256)
                 nc.vector.tensor_tensor(tile[:, cols], pair[0][:, cols], pair[1][:, cols], ALU.max)
-            run = width // PACK
-            rows = slice(c0 // PACK, c0 // PACK + run)
-            for u in range(P // run):
-                src = tile[run * u:run * u + run, :]
-                if t0 + u < 3:
-                    nc.sync.dma_start(m[t0 + u][rows, :], src)
-                else:
-                    for i in range(2):
-                        nc.sync.dma_start(m_half[i][3][rows, :], src[:, 256 * i:256 * i + 256])
+                for u in range(P // run):
+                    nc.sync.dma_start(m_half[i][t0 + u][rows, :], tile[run * u:run * u + run, cols])
 
         e0 = product(qa, "e0", TAPERED, nc.vector.tensor_copy)
         larger(neighbours(e0, 0), 0, 128, 0)

@@ -26,10 +26,14 @@ def tile_picked_edgecv_relu_p_kernel(tc, x_words, x_scales, w1, w2, w3_words, w3
     nc = tc.nc
     with ExitStack() as ctx:
         keep = ctx.enter_context(tc.tile_pool(name="keep", bufs=1))
+        late = ctx.enter_context(tc.tile_pool(name="late", bufs=1))
         psum = ctx.enter_context(tc.psum_pool(name="psum", bufs=1))
 
         def sb(shape, dtype, name, tag=None, bufs=1):
             return keep.tile(shape, dtype, name=name, tag=tag or name, bufs=bufs, align_bytes=64)
+
+        def placed(shape, dtype, name, kib):
+            return late.tile(shape, dtype, name=name, align_bytes=64, offset=int(kib * 1024))
 
         def load_list(src, name):
             tile = keep.tile(list(src.shape), U16, name=name)
@@ -41,74 +45,91 @@ def tile_picked_edgecv_relu_p_kernel(tc, x_words, x_scales, w1, w2, w3_words, w3
             nc.sync.dma_start(tile[:], x_words[z].rearrange("p c r -> p (c r)").bitcast(I32))
             return tile
 
-        def load_weight(w, z, c0, c1, name):
-            tile = sb([P, PACK, c1 - c0], F32, name)
+        def load_weight(w, z, c0, c1, name, kib=None):
+            tile = sb([P, PACK, c1 - c0], F32, name) if kib is None else placed([P, PACK, c1 - c0], F32, name, kib)
             nc.sync.dma_start(tile[:], w[z * 512:(z + 1) * 512, c0:c1].rearrange("(p j) c -> p j c", j=PACK))
             return tile
 
         def scalar_cast(dst, src):
             nc.scalar.activation(dst, src, ACT.Copy)
 
-        def quantise_weight(raws, name, codes_tag=None):
+        def gpsimd_cast(dst, src):
+            nc.gpsimd.tensor_scalar(dst, src, 1.0, 0.0, ALU.mult, ALU.add)
+
+        def quantise_weight(raws, name, codes_tag=None, plain=False):
             width = raws[0].shape[2]
             grouped = sb([P, len(raws), PACK, width // PACK, PACK], BF16, name + "_grouped")
             for z, raw in enumerate(raws):
-                scalar_cast(grouped[:, z].rearrange("p t m j -> p m j t"), raw[:].rearrange("p j (m t) -> p m j t", t=PACK))
+                if plain:
+                    gpsimd_cast(grouped[:, z].rearrange("p t m j -> p (t m) j"), raw[:].rearrange("p j c -> p c j"))
+                else:
+                    scalar_cast(grouped[:, z].rearrange("p t m j -> p m j t"), raw[:].rearrange("p j (m t) -> p m j t", t=PACK))
             codes = sb([P, len(raws) * width], U32, name + "_codes", tag=codes_tag)
             scales = sb([P, len(raws) * width], U8, name + "_scales")
             nc.vector.quantize_mx(out=codes[:].bitcast(FP8X4), scales=scales[:], in_=grouped[:].rearrange("p z t m j -> p (z t m j)"))
             return [(codes[:, i:i + P], scales[:, i:i + P]) for i in range(0, len(raws) * width, P)]
 
-        def gather_words(table, z, pieces, tag=None):
-            tile = sb([P, S], U32, "x_picked%d" % z, tag=tag)
+        def gather_words(table, name, pieces, tag=None):
+            base = pieces[0][0]
+            tile = sb([P, pieces[-1][1] - base], U32, name, tag=tag)
             for c0, c1 in pieces:
-                nc.vector.tensor_copy(tile[:, c0:c1], table[:].bitcast(U32).indirect(offs_sb[:, c0 // 16:c1 // 16]))
+                nc.vector.tensor_copy(tile[:, c0 - base:c1 - base], table[:].bitcast(U32).indirect(offs_sb[:, c0 // 16:c1 // 16]))
             return tile
 
-        def product(weights, name, pieces=HALVES, last_copy=nc.scalar.copy, tag=None):
-            rows = sb([P, S], F32, name, tag=tag)
+        def product(weights, name, pieces=HALVES, last_copy=nc.scalar.copy, kib=None):
+            rows = sb([P, S], F32, name) if kib is None else placed([P, S], F32, name, kib)
             for c0, c1 in pieces:
                 acc = psum.tile([P, c1 - c0], F32, name="acc", tag="acc", bufs=8)
                 for z in range(PASSES):
+                    words = picked0[:, c0:c1] if z == 0 else picked1[c0 // 512][:, c0 % 512:c0 % 512 + c1 - c0]
                     nc.tensor.matmul_mx(
                         out=acc[:], lhsT=weights[z][0].bitcast(FP8X4), lhsT_scale=weights[z][1],
-                        rhs=picked[z][:, c0:c1].bitcast(FP8X4), rhs_scale=picked_scales[4 * z:P, c0:c1],
+                        rhs=words.bitcast(FP8X4), rhs_scale=picked_scales[4 * z:P, c0:c1],
                         start=(z == 0), stop=(z == PASSES - 1))
                 (last_copy if c1 == S else nc.scalar.copy)(rows[:, c0:c1], acc[:])
             return rows
 
-        x_scale_table = sb([P, T], U8, "x_scale_table")
-        nc.vector.memset(x_scale_table[:].bitcast(I32), 0)
-        w3_scale = sb([P, N], U8, "w3_scale")
-        nc.vector.memset(w3_scale[:].bitcast(I32), 0)
-
-        table0 = load_words(0)
+        x_scale_table = placed([P, 2 * T], U8, "x_scale_table", 0)
+        nc.gpsimd.memset(x_scale_table[32:64, 0:T].bitcast(I32), 0)
+        nc.gpsimd.memset(x_scale_table[64:P, 0:T].bitcast(I32), 0)
+        for z in range(PASSES):
+            nc.sync.dma_start(x_scale_table[z:32:2, 0:T].bitcast(I32), x_scales[z].bitcast(I32))
         offs_sb = load_list(offs, "offs_sb")
-        for q in range(4):
-            nc.sync.dma_start(x_scale_table[32 * q:32 * q + 8, :].bitcast(I32), x_scales[:, 4 * q:4 * q + 4, :].bitcast(I32))
-        raw_a = [load_weight(w2, z, 0, 128, "raw_a%d" % z) for z in range(PASSES)]
-        table1 = load_words(1)
-        raw_b = [load_weight(w2, z, 128, 256, "raw_b%d" % z) for z in range(PASSES)]
+        table0 = load_words(0)
+        raw_a0 = load_weight(w2, 0, 0, 128, "raw_a0")
         pos1_sb = load_list(pos1, "pos1_sb")
         pos2_sb = load_list(pos2, "pos2_sb")
-        raw_c = [load_weight(w2, z, 256, H, "raw_c%d" % z) for z in range(PASSES)]
-        raw10 = load_weight(w1, 0, 0, H, "raw10")
-        raw11 = load_weight(w1, 1, 0, H, "raw11")
         cen_sb = load_list(cen, "cen_sb")
-        w3_code = sb([P, N], U32, "w3_code")
+        table1 = load_words(1)
+        raw_a1 = load_weight(w2, 1, 0, 128, "raw_a1")
+
+        scale_rows = placed([P, 25 * 1024], U8, "scale_rows", 4)
+        nc.vector.tensor_copy(scale_rows[:, 0:S], x_scale_table[:, 0:T].indirect(offs_sb[:]))
+        picked0 = gather_words(table0, "x_picked0", ((0, S),))
+        qa = quantise_weight([raw_a0], "wa0")
+        picked_scales = sb([P, S], U8, "picked_scales", tag="raw_a0")
+        for r in range(4):
+            nc.scalar.dma_start(picked_scales[r:P:4, :].bitcast(I32), scale_rows[2 * r:2 * r + 32, 0:S].bitcast(I32))
+
+        raw_b = [load_weight(w2, z, 128, 256, "raw_b%d" % z, 2 * z) for z in range(PASSES)]
+        raw_c = [load_weight(w2, z, 256, H, "raw_c%d" % z, 4 + 4 * z) for z in range(PASSES)]
+        raw10 = load_weight(w1, 0, 0, H, "raw10", 12)
+        raw11 = load_weight(w1, 1, 0, H, "raw11", 20)
+        w3_code = placed([P, N], U32, "w3_code", 28)
         nc.sync.dma_start(w3_code[:].bitcast(I32), w3_words[0].rearrange("p c r -> p (c r)").bitcast(I32))
+        w3_scale = placed([P, N], U8, "w3_scale", 28.5)
+        nc.vector.memset(w3_scale[:].bitcast(I32), 0)
         for q in range(4):
             nc.sync.dma_start(w3_scale[32 * q:32 * q + 4, :].bitcast(I32), w3_scales[0, 4 * q:4 * q + 4, :].bitcast(I32))
 
-        picked = [gather_words(table0, 0, ((0, S),))]
-        picked_scales = sb([P, S], U8, "picked_scales")
-        nc.vector.tensor_copy(picked_scales[:], x_scale_table[:].indirect(offs_sb[:]))
-        qa = quantise_weight(raw_a, "wa")
-        picked.append(gather_words(table1, 1, TAPERED, "wa_grouped"))
-        qb = quantise_weight(raw_b, "wb", "x_table1")
+        picked1 = [gather_words(table1, "x_picked1a", TAPERED[:1])]
+        qa = qa + quantise_weight([raw_a1], "wa1")
+        picked1.append(gather_words(table1, "x_picked1b", TAPERED[1:], "raw_a1"))
+        qb = quantise_weight(raw_b, "wb", "x_table1", plain=True)
 
-        edge = [sb([P, PACK, 256], F32, "edge%d" % (i,)) for i in range(2)]
-        m_half = [[sb([P, 256], F32, "larger%d_%d" % (i, t))[:] if (i, t) != (0, 3) else edge[1][:, 2, :] for t in range(4)] for i in range(2)]
+        edge = sb([P, PACK, V], F32, "edge")
+        m_full = [sb([P, V], F32, "larger%d" % (t,)) for t in range(4)]
+        m_half = [[m_full[t][:, 256 * i:256 * i + 256] if (i, t) != (0, 3) else edge[:, 2, 256:512] for t in range(4)] for i in range(2)]
 
         def neighbours(e_rows, i):
             first = sb([P, V], F32, "first%d" % (i,))
@@ -118,7 +139,7 @@ def tile_picked_edgecv_relu_p_kernel(tc, x_words, x_scales, w1, w2, w3_words, w3
                 nc.vector.tensor_copy(second[:, 256 * i:256 * i + 256], e_rows[:].indirect(pos2_sb[:, 16 * i:16 * i + 16]))
             return first, second
 
-        def larger(pair, c0, width, t0):
+        def larger(pair, c0, width, t0, plain=False):
             tile = sb([P, V], F32, "unplaced%d_%d" % (c0, t0))
             run = width // PACK
             rows = slice(c0 // PACK, c0 // PACK + run)
@@ -126,13 +147,13 @@ def tile_picked_edgecv_relu_p_kernel(tc, x_words, x_scales, w1, w2, w3_words, w3
                 cols = slice(256 * i, 256 * i + 256)
                 nc.vector.tensor_tensor(tile[:, cols], pair[0][:, cols], pair[1][:, cols], ALU.max)
                 for u in range(P // run):
-                    nc.sync.dma_start(m_half[i][t0 + u][rows, :], tile[run * u:run * u + run, cols])
+                    nc.sync.dma_start(m_half[i][t0 + u][rows, :], tile[u:P:PACK, cols] if plain else tile[run * u:run * u + run, cols])
 
         e0 = product(qa, "e0", TAPERED, nc.vector.tensor_copy)
         larger(neighbours(e0, 0), 0, 128, 0)
         qc = quantise_weight(raw_c, "wc")
-        e1 = product(qb, "e1", tag="raw_c0")
-        larger(neighbours(e1, 1), 128, 128, 0)
+        e1 = product(qb, "e1", kib=4)
+        larger(neighbours(e1, 1), 128, 128, 0, plain=True)
         q10 = quantise_weight([raw10], "w10")
         e2 = product([qc[0], qc[2]], "e2")
         larger(neighbours(e2, 2), 256, 256, 0)
@@ -141,8 +162,9 @@ def tile_picked_edgecv_relu_p_kernel(tc, x_words, x_scales, w1, w2, w3_words, w3
         larger(neighbours(e3, 3), 256, 256, 2)
         y = [product([q10[t], q11[t]], "y%d" % (t,)) for t in range(4)]
 
-        def add_centres(i, t):
-            nc.vector.tensor_tensor(edge[i][:, t, :], y[t][:].indirect(cen_sb[:, 16 * i:16 * i + 16]), m_half[i][t], ALU.add)
+        def add_centres(v0, v1, t):
+            larger_part = m_half[v0 // 256][t][:, v0 % 256:v0 % 256 + v1 - v0]
+            nc.vector.tensor_tensor(edge[:, t, v0:v1], y[t][:].indirect(cen_sb[:, v0 // 16:v1 // 16]), larger_part, ALU.add)
 
         def scalar_relu(dst, src):
             nc.scalar.activation(dst, src, ACT.Relu)
@@ -153,7 +175,7 @@ def tile_picked_edgecv_relu_p_kernel(tc, x_words, x_scales, w1, w2, w3_words, w3
         def project(v0, v1, relu):
             n = v1 - v0
             z = sb([P, n, PACK], BF16, "z%d" % v0)
-            sums = edge[v0 // 256][:, :, v0 % 256:v0 % 256 + n]
+            sums = edge[:, :, v0:v1]
             relu(z[:].rearrange("p (c i) t -> p c t i", i=4), sums.rearrange("p t (c i) -> p c t i", i=4))
             z_codes = sb([P, n], U32, "z_codes%d" % v0)
             z_scales = sb([P, n], U8, "z_scales%d" % v0)
@@ -165,10 +187,10 @@ def tile_picked_edgecv_relu_p_kernel(tc, x_words, x_scales, w1, w2, w3_words, w3
             nc.scalar.copy(res_sb[:], res[:])
             nc.sync.dma_start(out[:, v0:v1], res_sb[:])
 
-        for t in range(4):
-            add_centres(0, t)
-        for t in range(4):
-            add_centres(1, t)
+        for t in range(2):
+            nc.vector.tensor_tensor(edge[:, t, :], y[t][:].indirect(cen_sb[:]), m_full[t][:], ALU.add)
+        for v0, v1, t in ((0, 256, 2), (0, 256, 3), (256, 512, 2), (256, 384, 3), (384, 512, 3)):
+            add_centres(v0, v1, t)
         project(0, 256, scalar_relu)
         project(256, 384, scalar_relu)
         project(384, 512, vector_relu)

@@ -42,7 +42,7 @@ def tile_picked_edgecv_relu_p_kernel(tc, x_words, x_scales, w1, w2, w3_words, w3
 
         def load_words(z):
             tile = sb([P, T], I32, "x_table%d" % (z,))
-            nc.sync.dma_start(tile[:], x_words[z].rearrange("p c r -> p (c r)").bitcast(I32))
+            nc.sync.dma_start(tile[:, 0:T], x_words[z].rearrange("p c r -> p (c r)").bitcast(I32))
             return tile
 
         def load_weight(w, z, c0, c1, name, kib=None):
@@ -63,7 +63,9 @@ def tile_picked_edgecv_relu_p_kernel(tc, x_words, x_scales, w1, w2, w3_words, w3
                 if plain:
                     gpsimd_cast(grouped[:, z].rearrange("p t m j -> p (t m) j"), raw[:].rearrange("p j c -> p c j"))
                 else:
-                    scalar_cast(grouped[:, z].rearrange("p t m j -> p m j t"), raw[:].rearrange("p j (m t) -> p m j t", t=PACK))
+                    for m0 in range(0, width // PACK, 128):
+                        scalar_cast(grouped[:, z, :, m0:min(m0 + 128, width // PACK)].rearrange("p t m j -> p m j t"),
+                                    raw[:].rearrange("p j (m t) -> p m j t", t=PACK)[:, m0:min(m0 + 128, width // PACK)])
             codes = sb([P, len(raws) * width], U32, name + "_codes", tag=codes_tag)
             scales = sb([P, len(raws) * width], U8, name + "_scales")
             nc.vector.quantize_mx(out=codes[:].bitcast(FP8X4), scales=scales[:], in_=grouped[:].rearrange("p z t m j -> p (z t m j)"))
@@ -73,7 +75,7 @@ def tile_picked_edgecv_relu_p_kernel(tc, x_words, x_scales, w1, w2, w3_words, w3
             base = pieces[0][0]
             tile = sb([P, pieces[-1][1] - base], U32, name, tag=tag)
             for c0, c1 in pieces:
-                nc.vector.tensor_copy(tile[:, c0 - base:c1 - base], table[:].bitcast(U32).indirect(offs_sb[:, c0 // 16:c1 // 16]))
+                nc.vector.tensor_copy(tile[:, c0 - base:c1 - base], table[:, 0:T].bitcast(U32).indirect(offs_sb[:, c0 // 16:c1 // 16]))
             return tile
 
         def product(weights, name, pieces=HALVES, last_copy=nc.scalar.copy, kib=None):
@@ -81,29 +83,30 @@ def tile_picked_edgecv_relu_p_kernel(tc, x_words, x_scales, w1, w2, w3_words, w3
             for c0, c1 in pieces:
                 acc = psum.tile([P, c1 - c0], F32, name="acc", tag="acc", bufs=8)
                 for z in range(PASSES):
-                    words = picked0[:, c0:c1] if z == 0 else picked1[c0 // 512][:, c0 % 512:c0 % 512 + c1 - c0]
+                    words = (picked0, picked1)[z][:, c0:c1]
                     nc.tensor.matmul_mx(
                         out=acc[:], lhsT=weights[z][0].bitcast(FP8X4), lhsT_scale=weights[z][1],
                         rhs=words.bitcast(FP8X4), rhs_scale=picked_scales[4 * z:P, c0:c1],
                         start=(z == 0), stop=(z == PASSES - 1))
-                (last_copy if c1 == S else nc.scalar.copy)(rows[:, c0:c1], acc[:])
+                (last_copy if c0 >= 512 else nc.scalar.copy)(rows[:, c0:c1], acc[:])
             return rows
 
-        x_scale_table = placed([P, 2 * T], U8, "x_scale_table", 0)
+        x_scale_table = sb([P, T], U8, "x_scale_table")
         nc.gpsimd.memset(x_scale_table[32:64, 0:T].bitcast(I32), 0)
         nc.gpsimd.memset(x_scale_table[64:P, 0:T].bitcast(I32), 0)
         for z in range(PASSES):
             nc.sync.dma_start(x_scale_table[z:32:2, 0:T].bitcast(I32), x_scales[z].bitcast(I32))
         offs_sb = load_list(offs, "offs_sb")
-        table0 = load_words(0)
         raw_a0 = load_weight(w2, 0, 0, 128, "raw_a0")
+        table0 = load_words(0)
+        raw_a1 = placed([P, 16, PACK, 128], F32, "raw_a1", 0)[:, 0]
+        nc.sync.dma_start(raw_a1, w2[512:K, 0:128].rearrange("(p j) c -> p j c", j=PACK))
         pos1_sb = load_list(pos1, "pos1_sb")
         pos2_sb = load_list(pos2, "pos2_sb")
         cen_sb = load_list(cen, "cen_sb")
         table1 = load_words(1)
-        raw_a1 = load_weight(w2, 1, 0, 128, "raw_a1")
 
-        scale_rows = placed([P, 25 * 1024], U8, "scale_rows", 4)
+        scale_rows = sb([P, S], U8, "scale_rows")
         nc.vector.tensor_copy(scale_rows[:, 0:S], x_scale_table[:, 0:T].indirect(offs_sb[:]))
         picked0 = gather_words(table0, "x_picked0", ((0, S),))
         qa = quantise_weight([raw_a0], "wa0")
@@ -112,29 +115,28 @@ def tile_picked_edgecv_relu_p_kernel(tc, x_words, x_scales, w1, w2, w3_words, w3
             nc.scalar.dma_start(picked_scales[r:P:4, :].bitcast(I32), scale_rows[2 * r:2 * r + 32, 0:S].bitcast(I32))
 
         raw_b = [load_weight(w2, z, 128, 256, "raw_b%d" % z, 2 * z) for z in range(PASSES)]
-        raw_c = [load_weight(w2, z, 256, H, "raw_c%d" % z, 4 + 4 * z) for z in range(PASSES)]
-        raw10 = load_weight(w1, 0, 0, H, "raw10", 12)
-        raw11 = load_weight(w1, 1, 0, H, "raw11", 20)
-        w3_code = placed([P, N], U32, "w3_code", 28)
+        raw_c = [load_weight(w2, z, 256, H, "raw_c%d" % z, 6 + 4 * z) for z in range(PASSES)]
+        raw10 = load_weight(w1, 0, 0, H, "raw10", 14)
+        raw11 = load_weight(w1, 1, 0, H, "raw11", 22)
+        w3_code = placed([P, N], U32, "w3_code", 30)
         nc.sync.dma_start(w3_code[:].bitcast(I32), w3_words[0].rearrange("p c r -> p (c r)").bitcast(I32))
-        w3_scale = placed([P, N], U8, "w3_scale", 28.5)
+        w3_scale = placed([P, N], U8, "w3_scale", 30.5)
         nc.vector.memset(w3_scale[:].bitcast(I32), 0)
         for q in range(4):
             nc.sync.dma_start(w3_scale[32 * q:32 * q + 4, :].bitcast(I32), w3_scales[0, 4 * q:4 * q + 4, :].bitcast(I32))
 
-        picked1 = [gather_words(table1, "x_picked1a", TAPERED[:1])]
         qa = qa + quantise_weight([raw_a1], "wa1")
-        picked1.append(gather_words(table1, "x_picked1b", TAPERED[1:], "raw_a1"))
-        qb = quantise_weight(raw_b, "wb", "x_table1", plain=True)
+        picked1 = gather_words(table1, "x_picked1", TAPERED)
+        qb = quantise_weight(raw_b, "wb", "x_table1")
 
         edge = sb([P, PACK, V], F32, "edge")
         m_full = [sb([P, V], F32, "larger%d" % (t,)) for t in range(4)]
         m_half = [[m_full[t][:, 256 * i:256 * i + 256] if (i, t) != (0, 3) else edge[:, 2, 256:512] for t in range(4)] for i in range(2)]
 
-        def neighbours(e_rows, i):
-            first = sb([P, V], F32, "first%d" % (i,))
+        def neighbours(e_rows, i, first_kib=None, second_kib=None):
+            first = sb([P, V], F32, "first%d" % (i,)) if first_kib is None else placed([P, V], F32, "first%d" % (i,), first_kib)
             nc.vector.tensor_copy(first[:], e_rows[:].indirect(pos1_sb[:]))
-            second = sb([P, V], F32, "second%d" % (i,))
+            second = sb([P, V], F32, "second%d" % (i,)) if second_kib is None else placed([P, V], F32, "second%d" % (i,), second_kib)
             for i in range(2):
                 nc.vector.tensor_copy(second[:, 256 * i:256 * i + 256], e_rows[:].indirect(pos2_sb[:, 16 * i:16 * i + 16]))
             return first, second
@@ -149,16 +151,16 @@ def tile_picked_edgecv_relu_p_kernel(tc, x_words, x_scales, w1, w2, w3_words, w3
                 for u in range(P // run):
                     nc.sync.dma_start(m_half[i][t0 + u][rows, :], tile[u:P:PACK, cols] if plain else tile[run * u:run * u + run, cols])
 
-        e0 = product(qa, "e0", TAPERED, nc.vector.tensor_copy)
+        e0 = product(qa, "e0", TAPERED, nc.vector.tensor_copy, kib=2)
         larger(neighbours(e0, 0), 0, 128, 0)
+        e1 = product(qb, "e1", kib=6)
         qc = quantise_weight(raw_c, "wc")
-        e1 = product(qb, "e1", kib=4)
-        larger(neighbours(e1, 1), 128, 128, 0, plain=True)
+        larger(neighbours(e1, 1, first_kib=10), 128, 128, 0)
+        e2 = product([qc[0], qc[2]], "e2", kib=14)
         q10 = quantise_weight([raw10], "w10")
-        e2 = product([qc[0], qc[2]], "e2")
         larger(neighbours(e2, 2), 256, 256, 0)
+        e3 = product([qc[1], qc[3]], "e3", kib=22)
         q11 = quantise_weight([raw11], "w11")
-        e3 = product([qc[1], qc[3]], "e3")
         larger(neighbours(e3, 3), 256, 256, 2)
         y = [product([q10[t], q11[t]], "y%d" % (t,)) for t in range(4)]
 

@@ -56,16 +56,15 @@ def tile_picked_edgecv_relu_p_kernel(tc, x_words, x_scales, w1, w2, w3_words, w3
         def gpsimd_cast(dst, src):
             nc.gpsimd.tensor_scalar(dst, src, 1.0, 0.0, ALU.mult, ALU.add)
 
-        def quantise_weight(raws, name, codes_tag=None, plain=False):
+        def quantise_weight(raws, name, codes_tag=None, shared=False, grouped_tag=None):
             width = raws[0].shape[2]
-            grouped = sb([P, len(raws), PACK, width // PACK, PACK], BF16, name + "_grouped")
+            grouped = sb([P, len(raws), PACK, width // PACK, PACK], BF16, name + "_grouped", tag=grouped_tag)
             for z, raw in enumerate(raws):
-                if plain:
-                    gpsimd_cast(grouped[:, z].rearrange("p t m j -> p (t m) j"), raw[:].rearrange("p j c -> p c j"))
+                if shared:
+                    gpsimd_cast(grouped[:, z, 0], raw[:].rearrange("p j (m t) -> p t m j", t=PACK)[:, 0])
+                    scalar_cast(grouped[:, z, 1:4].rearrange("p t m j -> p m j t"), raw[:].rearrange("p j (m t) -> p m j t", t=PACK)[:, :, :, 1:4])
                 else:
-                    for m0 in range(0, width // PACK, 128):
-                        scalar_cast(grouped[:, z, :, m0:min(m0 + 128, width // PACK)].rearrange("p t m j -> p m j t"),
-                                    raw[:].rearrange("p j (m t) -> p m j t", t=PACK)[:, m0:min(m0 + 128, width // PACK)])
+                    scalar_cast(grouped[:, z].rearrange("p t m j -> p m j t"), raw[:].rearrange("p j (m t) -> p m j t", t=PACK))
             codes = sb([P, len(raws) * width], U32, name + "_codes", tag=codes_tag)
             scales = sb([P, len(raws) * width], U8, name + "_scales")
             nc.vector.quantize_mx(out=codes[:].bitcast(FP8X4), scales=scales[:], in_=grouped[:].rearrange("p z t m j -> p (z t m j)"))
@@ -157,10 +156,10 @@ def tile_picked_edgecv_relu_p_kernel(tc, x_words, x_scales, w1, w2, w3_words, w3
         qc = quantise_weight(raw_c, "wc")
         larger(neighbours(e1, 1, first_kib=10), 128, 128, 0)
         e2 = product([qc[0], qc[2]], "e2", kib=14)
-        q10 = quantise_weight([raw10], "w10")
+        q10 = quantise_weight([raw10], "w10", shared=True, grouped_tag="wc_grouped")
         larger(neighbours(e2, 2), 256, 256, 0)
         e3 = product([qc[1], qc[3]], "e3", kib=22)
-        q11 = quantise_weight([raw11], "w11")
+        q11 = quantise_weight([raw11], "w11", shared=True, grouped_tag="wc_grouped")
         larger(neighbours(e3, 3), 256, 256, 2)
         y = [product([q10[t], q11[t]], "y%d" % (t,)) for t in range(4)]
 

@@ -90,29 +90,26 @@ def tile_picked_edgecv_relu_p_kernel(tc, x_words, x_scales, w1, w2, w3_words, w3
                 (last_copy if c0 >= 512 else nc.scalar.copy)(rows[:, c0:c1], acc[:])
             return rows
 
-        x_scale_table = sb([P, T], U8, "x_scale_table")
+        x_scale_table = placed([P, 33 * 1024], U8, "x_scale_table", 0)
         nc.gpsimd.memset(x_scale_table[32:64, 0:T].bitcast(I32), 0)
         nc.gpsimd.memset(x_scale_table[64:P, 0:T].bitcast(I32), 0)
         for z in range(PASSES):
             nc.sync.dma_start(x_scale_table[z:32:2, 0:T].bitcast(I32), x_scales[z].bitcast(I32))
         offs_sb = load_list(offs, "offs_sb")
-        raw_a0 = load_weight(w2, 0, 0, 128, "raw_a0")
         table0 = load_words(0)
-        raw_a1 = placed([P, 16, PACK, 128], F32, "raw_a1", 0)[:, 0]
-        nc.sync.dma_start(raw_a1, w2[512:K, 0:128].rearrange("(p j) c -> p j c", j=PACK))
+        raw_a0 = load_weight(w2, 0, 0, 128, "raw_a0")
         pos1_sb = load_list(pos1, "pos1_sb")
         pos2_sb = load_list(pos2, "pos2_sb")
         cen_sb = load_list(cen, "cen_sb")
         table1 = load_words(1)
 
         scale_rows = sb([P, S], U8, "scale_rows")
-        nc.vector.tensor_copy(scale_rows[:, 0:S], x_scale_table[:, 0:T].indirect(offs_sb[:]))
-        picked0 = gather_words(table0, "x_picked0", ((0, S),))
-        qa = quantise_weight([raw_a0], "wa0")
-        picked_scales = sb([P, S], U8, "picked_scales", tag="raw_a0")
+        nc.vector.tensor_copy(scale_rows[:], x_scale_table[:, 0:T].indirect(offs_sb[:]))
+        picked_scales = sb([P, S], U8, "picked_scales")
         for r in range(4):
-            nc.scalar.dma_start(picked_scales[r:P:4, :].bitcast(I32), scale_rows[2 * r:2 * r + 32, 0:S].bitcast(I32))
+            nc.sync.dma_start(picked_scales[r:P:4, :].bitcast(I32), scale_rows[2 * r:2 * r + 32, :].bitcast(I32))
 
+        raw_a1 = load_weight(w2, 1, 0, 128, "raw_a1", 31)
         raw_b = [load_weight(w2, z, 128, 256, "raw_b%d" % z, 2 * z) for z in range(PASSES)]
         raw_c = [load_weight(w2, z, 256, H, "raw_c%d" % z, 6 + 4 * z) for z in range(PASSES)]
         raw10 = load_weight(w1, 0, 0, H, "raw10", 14)
@@ -124,29 +121,35 @@ def tile_picked_edgecv_relu_p_kernel(tc, x_words, x_scales, w1, w2, w3_words, w3
         for q in range(4):
             nc.sync.dma_start(w3_scale[32 * q:32 * q + 4, :].bitcast(I32), w3_scales[0, 4 * q:4 * q + 4, :].bitcast(I32))
 
-        qa = qa + quantise_weight([raw_a1], "wa1")
+        picked0 = gather_words(table0, "x_picked0", ((0, S),))
+        qa = quantise_weight([raw_a0], "wa0")
         picked1 = gather_words(table1, "x_picked1", TAPERED)
+        qa = qa + quantise_weight([raw_a1], "wa1")
         qb = quantise_weight(raw_b, "wb", "x_table1")
 
         edge = sb([P, PACK, V], F32, "edge")
         m_full = [sb([P, V], F32, "larger%d" % (t,)) for t in range(4)]
         m_half = [[m_full[t][:, 256 * i:256 * i + 256] if (i, t) != (0, 3) else edge[:, 2, 256:512] for t in range(4)] for i in range(2)]
 
-        def neighbours(e_rows, i, first_kib=None, second_kib=None):
+        def neighbours(e_rows, i, first_kib=None, second_kib=None, step=256):
             first = sb([P, V], F32, "first%d" % (i,)) if first_kib is None else placed([P, V], F32, "first%d" % (i,), first_kib)
             nc.vector.tensor_copy(first[:], e_rows[:].indirect(pos1_sb[:]))
             second = sb([P, V], F32, "second%d" % (i,)) if second_kib is None else placed([P, V], F32, "second%d" % (i,), second_kib)
-            for i in range(2):
-                nc.vector.tensor_copy(second[:, 256 * i:256 * i + 256], e_rows[:].indirect(pos2_sb[:, 16 * i:16 * i + 16]))
+            for v0 in range(0, V, step):
+                nc.vector.tensor_copy(second[:, v0:v0 + step], e_rows[:].indirect(pos2_sb[:, v0 // 16:(v0 + step) // 16]))
             return first, second
 
-        def larger(pair, c0, width, t0, plain=False):
-            tile = sb([P, V], F32, "unplaced%d_%d" % (c0, t0))
+        def larger(pair, c0, width, t0, plain=False, kib=None, whole=False):
+            name = "unplaced%d_%d" % (c0, t0)
+            tile = sb([P, V], F32, name) if kib is None else placed([P, V], F32, name, kib)
             run = width // PACK
             rows = slice(c0 // PACK, c0 // PACK + run)
+            if whole:
+                nc.vector.tensor_tensor(tile[:], pair[0][:], pair[1][:], ALU.max)
             for i in range(2):
                 cols = slice(256 * i, 256 * i + 256)
-                nc.vector.tensor_tensor(tile[:, cols], pair[0][:, cols], pair[1][:, cols], ALU.max)
+                if not whole:
+                    nc.vector.tensor_tensor(tile[:, cols], pair[0][:, cols], pair[1][:, cols], ALU.max)
                 for u in range(P // run):
                     nc.sync.dma_start(m_half[i][t0 + u][rows, :], tile[u:P:PACK, cols] if plain else tile[run * u:run * u + run, cols])
 
@@ -154,12 +157,14 @@ def tile_picked_edgecv_relu_p_kernel(tc, x_words, x_scales, w1, w2, w3_words, w3
         larger(neighbours(e0, 0), 0, 128, 0)
         e1 = product(qb, "e1", kib=6)
         qc = quantise_weight(raw_c, "wc")
-        larger(neighbours(e1, 1, first_kib=10), 128, 128, 0)
+        pair1 = neighbours(e1, 1, first_kib=10, step=V)
         e2 = product([qc[0], qc[2]], "e2", kib=14)
         q10 = quantise_weight([raw10], "w10", shared=True, grouped_tag="wc_grouped")
-        larger(neighbours(e2, 2), 256, 256, 0)
+        larger(pair1, 128, 128, 0, kib=18, whole=True)
+        pair2 = neighbours(e2, 2, step=V)
         e3 = product([qc[1], qc[3]], "e3", kib=22)
         q11 = quantise_weight([raw11], "w11", shared=True, grouped_tag="wc_grouped")
+        larger(pair2, 256, 256, 0, kib=26, whole=True)
         larger(neighbours(e3, 3), 256, 256, 2)
         y = [product([q10[t], q11[t]], "y%d" % (t,)) for t in range(4)]
 
@@ -173,11 +178,12 @@ def tile_picked_edgecv_relu_p_kernel(tc, x_words, x_scales, w1, w2, w3_words, w3
         def vector_relu(dst, src):
             nc.vector.tensor_scalar_max(dst, src, 0.0)
 
-        def project(v0, v1, relu):
+        def project(v0, v1, relu, copy=nc.scalar.copy):
             n = v1 - v0
             z = sb([P, n, PACK], BF16, "z%d" % v0)
-            sums = edge[:, :, v0:v1]
-            relu(z[:].rearrange("p (c i) t -> p c t i", i=4), sums.rearrange("p t (c i) -> p c t i", i=4))
+            for u0 in range(0, n, 128):
+                sums = edge[:, :, v0 + u0:v0 + u0 + 128]
+                relu(z[:, u0:u0 + 128].rearrange("p (c i) t -> p c t i", i=4), sums.rearrange("p t (c i) -> p c t i", i=4))
             z_codes = sb([P, n], U32, "z_codes%d" % v0)
             z_scales = sb([P, n], U8, "z_scales%d" % v0)
             nc.vector.quantize_mx(out=z_codes[:].bitcast(FP8X4), scales=z_scales[:], in_=z[:].rearrange("p c t -> p (c t)"))
@@ -185,13 +191,13 @@ def tile_picked_edgecv_relu_p_kernel(tc, x_words, x_scales, w1, w2, w3_words, w3
             nc.tensor.matmul_mx(out=res[:], lhsT=w3_code[:].bitcast(FP8X4), lhsT_scale=w3_scale[:],
                                 rhs=z_codes[:].bitcast(FP8X4), rhs_scale=z_scales[:], start=True, stop=True)
             res_sb = sb([P, n], F32, "res_sb%d" % v0)
-            nc.scalar.copy(res_sb[:], res[:])
+            copy(res_sb[:], res[:])
             nc.sync.dma_start(out[:, v0:v1], res_sb[:])
 
         for t in range(2):
             nc.vector.tensor_tensor(edge[:, t, :], y[t][:].indirect(cen_sb[:]), m_full[t][:], ALU.add)
-        for v0, v1, t in ((0, 256, 2), (0, 256, 3), (256, 512, 2), (256, 384, 3), (384, 512, 3)):
+        for v0, v1, t in ((0, 256, 2), (0, 128, 3), (128, 256, 3), (256, 512, 2), (256, 384, 3), (384, 512, 3)):
             add_centres(v0, v1, t)
         project(0, 256, scalar_relu)
         project(256, 384, scalar_relu)
-        project(384, 512, vector_relu)
+        project(384, 512, vector_relu, nc.vector.tensor_copy)

@@ -56,9 +56,10 @@ def tile_picked_edgecv_relu_p_kernel(tc, x_words, x_scales, w1, w2, w3_words, w3
         def gpsimd_cast(dst, src):
             nc.gpsimd.tensor_scalar(dst, src, 1.0, 0.0, ALU.mult, ALU.add)
 
-        def quantise_weight(raws, name, codes_tag=None, shared=False, grouped_tag=None):
+        def quantise_weight(raws, name, codes_tag=None, shared=False, grouped_tag=None, kib=None):
             width = raws[0].shape[2]
-            grouped = sb([P, len(raws), PACK, width // PACK, PACK], BF16, name + "_grouped", tag=grouped_tag)
+            shape = [P, len(raws), PACK, width // PACK, PACK]
+            grouped = sb(shape, BF16, name + "_grouped", tag=grouped_tag) if kib is None else placed(shape, BF16, name + "_grouped", kib)
             for z, raw in enumerate(raws):
                 if shared:
                     gpsimd_cast(grouped[:, z, 0], raw[:].rearrange("p j (m t) -> p t m j", t=PACK)[:, 0])
@@ -82,7 +83,7 @@ def tile_picked_edgecv_relu_p_kernel(tc, x_words, x_scales, w1, w2, w3_words, w3
             for c0, c1 in pieces:
                 acc = psum.tile([P, c1 - c0], F32, name="acc", tag="acc", bufs=8)
                 for z in range(PASSES):
-                    words = (picked0, picked1)[z][:, c0:c1]
+                    words = picked0[:, c0:c1] if z == 0 else picked1[:] if c0 == 0 else picked2[:, c0 - 512:c1 - 512]
                     nc.tensor.matmul_mx(
                         out=acc[:], lhsT=weights[z][0].bitcast(FP8X4), lhsT_scale=weights[z][1],
                         rhs=words.bitcast(FP8X4), rhs_scale=picked_scales[4 * z:P, c0:c1],
@@ -90,9 +91,9 @@ def tile_picked_edgecv_relu_p_kernel(tc, x_words, x_scales, w1, w2, w3_words, w3
                 (last_copy if c0 >= 512 else nc.scalar.copy)(rows[:, c0:c1], acc[:])
             return rows
 
-        x_scale_table = placed([P, 33 * 1024], U8, "x_scale_table", 0)
-        nc.gpsimd.memset(x_scale_table[32:64, 0:T].bitcast(I32), 0)
-        nc.gpsimd.memset(x_scale_table[64:P, 0:T].bitcast(I32), 0)
+        x_scale_table = placed([P, 50 * 1024], U8, "x_scale_table", 0)
+        nc.vector.memset(x_scale_table[32:64, 0:T].bitcast(I32), 0)
+        nc.vector.memset(x_scale_table[64:P, 0:T].bitcast(I32), 0)
         for z in range(PASSES):
             nc.sync.dma_start(x_scale_table[z:32:2, 0:T].bitcast(I32), x_scales[z].bitcast(I32))
         offs_sb = load_list(offs, "offs_sb")
@@ -102,6 +103,7 @@ def tile_picked_edgecv_relu_p_kernel(tc, x_words, x_scales, w1, w2, w3_words, w3
         pos2_sb = load_list(pos2, "pos2_sb")
         cen_sb = load_list(cen, "cen_sb")
         table1 = load_words(1)
+        raw_a1 = load_weight(w2, 1, 0, 128, "raw_a1")
 
         scale_rows = sb([P, S], U8, "scale_rows")
         nc.vector.tensor_copy(scale_rows[:], x_scale_table[:, 0:T].indirect(offs_sb[:]))
@@ -109,9 +111,8 @@ def tile_picked_edgecv_relu_p_kernel(tc, x_words, x_scales, w1, w2, w3_words, w3
         for r in range(4):
             nc.sync.dma_start(picked_scales[r:P:4, :].bitcast(I32), scale_rows[2 * r:2 * r + 32, :].bitcast(I32))
 
-        raw_a1 = load_weight(w2, 1, 0, 128, "raw_a1", 31)
         raw_b = [load_weight(w2, z, 128, 256, "raw_b%d" % z, 2 * z) for z in range(PASSES)]
-        raw_c = [load_weight(w2, z, 256, H, "raw_c%d" % z, 6 + 4 * z) for z in range(PASSES)]
+        raw_c = [load_weight(w2, z, 256, H, "raw_c%d" % z, (34, 44)[z]) for z in range(PASSES)]
         raw10 = load_weight(w1, 0, 0, H, "raw10", 14)
         raw11 = load_weight(w1, 1, 0, H, "raw11", 22)
         w3_code = placed([P, N], U32, "w3_code", 30)
@@ -123,49 +124,56 @@ def tile_picked_edgecv_relu_p_kernel(tc, x_words, x_scales, w1, w2, w3_words, w3
 
         picked0 = gather_words(table0, "x_picked0", ((0, S),))
         qa = quantise_weight([raw_a0], "wa0")
-        picked1 = gather_words(table1, "x_picked1", TAPERED)
+        picked1 = gather_words(table1, "x_picked1", TAPERED[0:1])
         qa = qa + quantise_weight([raw_a1], "wa1")
-        qb = quantise_weight(raw_b, "wb", "x_table1")
+        picked2 = gather_words(table1, "x_picked2", TAPERED[1:3], tag="raw_a1")
+        qb = quantise_weight(raw_b[0:1], "wb0", "x_table1")
 
         edge = sb([P, PACK, V], F32, "edge")
         m_full = [sb([P, V], F32, "larger%d" % (t,)) for t in range(4)]
         m_half = [[m_full[t][:, 256 * i:256 * i + 256] if (i, t) != (0, 3) else edge[:, 2, 256:512] for t in range(4)] for i in range(2)]
 
-        def neighbours(e_rows, i, first_kib=None, second_kib=None, step=256):
-            first = sb([P, V], F32, "first%d" % (i,)) if first_kib is None else placed([P, V], F32, "first%d" % (i,), first_kib)
-            nc.vector.tensor_copy(first[:], e_rows[:].indirect(pos1_sb[:]))
-            second = sb([P, V], F32, "second%d" % (i,)) if second_kib is None else placed([P, V], F32, "second%d" % (i,), second_kib)
+        def fetch(e_rows, places, name, kib=None, step=V):
+            tile = sb([P, V], F32, name) if kib is None else placed([P, V], F32, name, kib)
             for v0 in range(0, V, step):
-                nc.vector.tensor_copy(second[:, v0:v0 + step], e_rows[:].indirect(pos2_sb[:, v0 // 16:(v0 + step) // 16]))
-            return first, second
+                nc.vector.tensor_copy(tile[:, v0:v0 + step], e_rows[:].indirect(places[:, v0 // 16:(v0 + step) // 16]))
+            return tile
 
-        def larger(pair, c0, width, t0, plain=False, kib=None, whole=False):
+        def larger(first, second, c0, width, t0, kib=None, step=V):
             name = "unplaced%d_%d" % (c0, t0)
             tile = sb([P, V], F32, name) if kib is None else placed([P, V], F32, name, kib)
             run = width // PACK
             rows = slice(c0 // PACK, c0 // PACK + run)
-            if whole:
-                nc.vector.tensor_tensor(tile[:], pair[0][:], pair[1][:], ALU.max)
-            for i in range(2):
-                cols = slice(256 * i, 256 * i + 256)
-                if not whole:
-                    nc.vector.tensor_tensor(tile[:, cols], pair[0][:, cols], pair[1][:, cols], ALU.max)
+            for v0 in range(0, V, step):
+                nc.vector.tensor_tensor(tile[:, v0:v0 + step], first[:, v0:v0 + step], second[:, v0:v0 + step], ALU.max)
                 for u in range(P // run):
-                    nc.sync.dma_start(m_half[i][t0 + u][rows, :], tile[u:P:PACK, cols] if plain else tile[run * u:run * u + run, cols])
+                    if step == V and t0 + u < 3:
+                        nc.sync.dma_start(m_full[t0 + u][rows, :], tile[run * u:run * u + run, :])
+                    else:
+                        for i in range(v0 // 256, (v0 + step) // 256):
+                            nc.sync.dma_start(m_half[i][t0 + u][rows, :], tile[run * u:run * u + run, 256 * i:256 * i + 256])
 
-        e0 = product(qa, "e0", TAPERED, nc.vector.tensor_copy, kib=2)
-        larger(neighbours(e0, 0), 0, 128, 0)
-        e1 = product(qb, "e1", kib=6)
-        qc = quantise_weight(raw_c, "wc")
-        pair1 = neighbours(e1, 1, first_kib=10, step=V)
+        e0 = product([qa[0], qa[1]], "e0", TAPERED, nc.vector.tensor_copy)
+        qb = qb + quantise_weight(raw_b[1:2], "wb1")
+        first0 = fetch(e0, pos1_sb, "first0", 3)
+        second0 = fetch(e0, pos2_sb, "second0", 1)
+        qc = quantise_weight(raw_c[0:1], "wc0")
+        larger(first0, second0, 0, 128, 0, kib=33)
+        qc = qc + quantise_weight(raw_c[1:2], "wc1")
+        e1 = product(qb, "e1", kib=47)
+        first1 = fetch(e1, pos1_sb, "first1")
+        second1 = fetch(e1, pos2_sb, "second1")
         e2 = product([qc[0], qc[2]], "e2", kib=14)
-        q10 = quantise_weight([raw10], "w10", shared=True, grouped_tag="wc_grouped")
-        larger(pair1, 128, 128, 0, kib=18, whole=True)
-        pair2 = neighbours(e2, 2, step=V)
+        q10 = quantise_weight([raw10], "w10", shared=True, grouped_tag="wc1_grouped")
+        larger(first1, second1, 128, 128, 0, kib=18)
+        first2 = fetch(e2, pos1_sb, "first2")
+        second2 = fetch(e2, pos2_sb, "second2")
         e3 = product([qc[1], qc[3]], "e3", kib=22)
-        q11 = quantise_weight([raw11], "w11", shared=True, grouped_tag="wc_grouped")
-        larger(pair2, 256, 256, 0, kib=26, whole=True)
-        larger(neighbours(e3, 3), 256, 256, 2)
+        q11 = quantise_weight([raw11], "w11", shared=True, grouped_tag="wc1_grouped")
+        larger(first2, second2, 256, 256, 0, kib=26)
+        first3 = fetch(e3, pos1_sb, "first3")
+        second3 = fetch(e3, pos2_sb, "second3", step=256)
+        larger(first3, second3, 256, 256, 2, step=256)
         y = [product([q10[t], q11[t]], "y%d" % (t,)) for t in range(4)]
 
         def add_centres(v0, v1, t):
@@ -182,8 +190,8 @@ def tile_picked_edgecv_relu_p_kernel(tc, x_words, x_scales, w1, w2, w3_words, w3
             n = v1 - v0
             z = sb([P, n, PACK], BF16, "z%d" % v0)
             for u0 in range(0, n, 128):
-                sums = edge[:, :, v0 + u0:v0 + u0 + 128]
-                relu(z[:, u0:u0 + 128].rearrange("p (c i) t -> p c t i", i=4), sums.rearrange("p t (c i) -> p c t i", i=4))
+                sums = edge[:, :, v0 + u0:min(v0 + u0 + 128, v1)]
+                relu(z[:, u0:min(u0 + 128, n)].rearrange("p (c i) t -> p c t i", i=4), sums.rearrange("p t (c i) -> p c t i", i=4))
             z_codes = sb([P, n], U32, "z_codes%d" % v0)
             z_scales = sb([P, n], U8, "z_scales%d" % v0)
             nc.vector.quantize_mx(out=z_codes[:].bitcast(FP8X4), scales=z_scales[:], in_=z[:].rearrange("p c t -> p (c t)"))
@@ -196,8 +204,9 @@ def tile_picked_edgecv_relu_p_kernel(tc, x_words, x_scales, w1, w2, w3_words, w3
 
         for t in range(2):
             nc.vector.tensor_tensor(edge[:, t, :], y[t][:].indirect(cen_sb[:]), m_full[t][:], ALU.add)
-        for v0, v1, t in ((0, 256, 2), (0, 128, 3), (128, 256, 3), (256, 512, 2), (256, 384, 3), (384, 512, 3)):
+        for v0, v1, t in ((0, 256, 2), (0, 128, 3), (128, 256, 3), (256, 384, 2), (256, 384, 3), (384, 512, 2), (384, 448, 3), (448, 512, 3)):
             add_centres(v0, v1, t)
         project(0, 256, scalar_relu)
         project(256, 384, scalar_relu)
-        project(384, 512, vector_relu, nc.vector.tensor_copy)
+        project(384, 448, scalar_relu)
+        project(448, 512, vector_relu, nc.vector.tensor_copy)

@@ -71,6 +71,19 @@ def tile_picked_edgecv_relu_p_kernel(tc, x_words, x_scales, w1, w2, w3_words, w3
             nc.vector.quantize_mx(out=codes[:].bitcast(FP8X4), scales=scales[:], in_=grouped[:].rearrange("p z t m j -> p (z t m j)"))
             return [(codes[:, i:i + P], scales[:, i:i + P]) for i in range(0, len(raws) * width, P)]
 
+        def quantise_chunk(raw, name, codes_tag=None):
+            width = raw.shape[2]
+            tiles = width // P
+            grouped = sb([P, width, PACK], BF16, name + "_grouped")
+            if tiles == 1:
+                scalar_cast(grouped[:].rearrange("p (m t) j -> p m j t", t=PACK), raw[:].rearrange("p j (m t) -> p m j t", t=PACK))
+            else:
+                nc.scalar.copy(grouped[:].rearrange("p (u m e) j -> p m j u e", u=2, e=2), raw[:].rearrange("p j (m u e) -> p m j u e", u=2, e=2))
+            codes = sb([P, width], U32, name + "_codes", tag=codes_tag)
+            scales = sb([P, width], U8, name + "_scales")
+            nc.vector.quantize_mx(out=codes[:].bitcast(FP8X4), scales=scales[:], in_=grouped[:].rearrange("p c j -> p (c j)"))
+            return [(codes[:, i:i + P], scales[:, i:i + P]) for i in range(0, width, P)]
+
         def gather_words(table, name, pieces, tag=None):
             base = pieces[0][0]
             tile = sb([P, pieces[-1][1] - base], U32, name, tag=tag)
@@ -123,11 +136,11 @@ def tile_picked_edgecv_relu_p_kernel(tc, x_words, x_scales, w1, w2, w3_words, w3
             nc.sync.dma_start(w3_scale[32 * q:32 * q + 4, :].bitcast(I32), w3_scales[0, 4 * q:4 * q + 4, :].bitcast(I32))
 
         picked0 = gather_words(table0, "x_picked0", ((0, S),))
-        qa = quantise_weight([raw_a0], "wa0")
+        qa = quantise_chunk(raw_a0, "wa0")
         picked1 = gather_words(table1, "x_picked1", TAPERED[0:1])
-        qa = qa + quantise_weight([raw_a1], "wa1")
+        qa = qa + quantise_chunk(raw_a1, "wa1")
         picked2 = gather_words(table1, "x_picked2", TAPERED[1:3], tag="raw_a1")
-        qb = quantise_weight(raw_b[0:1], "wb0", "x_table1")
+        qb = quantise_chunk(raw_b[0], "wb0", "x_table1")
 
         edge = sb([P, PACK, V], F32, "edge")
         m_full = [sb([P, V], F32, "larger%d" % (t,)) for t in range(4)]
@@ -148,18 +161,18 @@ def tile_picked_edgecv_relu_p_kernel(tc, x_words, x_scales, w1, w2, w3_words, w3
                 nc.vector.tensor_tensor(tile[:, v0:v0 + step], first[:, v0:v0 + step], second[:, v0:v0 + step], ALU.max)
                 for u in range(P // run):
                     if step == V and t0 + u < 3:
-                        nc.sync.dma_start(m_full[t0 + u][rows, :], tile[run * u:run * u + run, :])
+                        nc.sync.dma_start(m_full[t0 + u][rows, :], tile[u:P:P // run, :])
                     else:
                         for i in range(v0 // 256, (v0 + step) // 256):
-                            nc.sync.dma_start(m_half[i][t0 + u][rows, :], tile[run * u:run * u + run, 256 * i:256 * i + 256])
+                            nc.sync.dma_start(m_half[i][t0 + u][rows, :], tile[u:P:P // run, 256 * i:256 * i + 256])
 
         e0 = product([qa[0], qa[1]], "e0", TAPERED, nc.vector.tensor_copy)
-        qb = qb + quantise_weight(raw_b[1:2], "wb1")
+        qb = qb + quantise_chunk(raw_b[1], "wb1")
         first0 = fetch(e0, pos1_sb, "first0", 3)
         second0 = fetch(e0, pos2_sb, "second0", 1)
-        qc = quantise_weight(raw_c[0:1], "wc0")
+        qc = quantise_chunk(raw_c[0], "wc0")
         larger(first0, second0, 0, 128, 0, kib=33)
-        qc = qc + quantise_weight(raw_c[1:2], "wc1")
+        qc = qc + quantise_chunk(raw_c[1], "wc1")
         e1 = product(qb, "e1", kib=47)
         first1 = fetch(e1, pos1_sb, "first1")
         second1 = fetch(e1, pos2_sb, "second1")

@@ -108,7 +108,7 @@ def tile_picked_edgecv_relu_p_kernel(tc, x_words, x_scales, w1, w2, w3_words, w3
         nc.vector.memset(x_scale_table[32:64, 0:T].bitcast(I32), 0)
         nc.vector.memset(x_scale_table[64:P, 0:T].bitcast(I32), 0)
         for z in range(PASSES):
-            nc.sync.dma_start(x_scale_table[z:32:2, 0:T].bitcast(I32), x_scales[z].bitcast(I32))
+            (nc.scalar, nc.sync)[z].dma_start(x_scale_table[z:32:2, 0:T].bitcast(I32), x_scales[z].bitcast(I32))
         offs_sb = load_list(offs, "offs_sb")
         table0 = load_words(0)
         raw_a0 = load_weight(w2, 0, 0, 128, "raw_a0")
@@ -199,6 +199,8 @@ def tile_picked_edgecv_relu_p_kernel(tc, x_words, x_scales, w1, w2, w3_words, w3
         def vector_relu(dst, src):
             nc.vector.tensor_scalar_max(dst, src, 0.0)
 
+        res_sb = sb([P, V], F32, "res_sb")
+
         def project(v0, v1, relu, copy=nc.scalar.copy):
             n = v1 - v0
             z = sb([P, n, PACK], BF16, "z%d" % v0)
@@ -211,15 +213,16 @@ def tile_picked_edgecv_relu_p_kernel(tc, x_words, x_scales, w1, w2, w3_words, w3
             res = psum.tile([P, n], F32, name="res", tag="acc", bufs=8)
             nc.tensor.matmul_mx(out=res[:], lhsT=w3_code[:].bitcast(FP8X4), lhsT_scale=w3_scale[:],
                                 rhs=z_codes[:].bitcast(FP8X4), rhs_scale=z_scales[:], start=True, stop=True)
-            res_sb = sb([P, n], F32, "res_sb%d" % v0)
-            copy(res_sb[:], res[:])
-            nc.sync.dma_start(out[:, v0:v1], res_sb[:])
+            copy(res_sb[:, v0:v1], res[:])
 
         for t in range(2):
             nc.vector.tensor_tensor(edge[:, t, :], y[t][:].indirect(cen_sb[:]), m_full[t][:], ALU.add)
         for v0, v1, t in ((0, 256, 2), (0, 128, 3), (128, 256, 3), (256, 384, 2), (256, 384, 3), (384, 512, 2), (384, 448, 3), (448, 512, 3)):
             add_centres(v0, v1, t)
         project(0, 256, scalar_relu)
+        nc.sync.dma_start(out[:, 0:256], res_sb[:, 0:256])
         project(256, 384, scalar_relu)
+        nc.sync.dma_start(out[:, 256:384], res_sb[:, 256:384])
         project(384, 448, scalar_relu)
         project(448, 512, vector_relu, nc.vector.tensor_copy)
+        nc.sync.dma_start(out[:, 384:V], res_sb[:, 384:V])

@@ -135,7 +135,11 @@ def tile_picked_edgecv_relu_p_kernel(tc, x_words, x_scales, w1, w2, w3_words, w3
         for q in range(4):
             nc.sync.dma_start(w3_scale[32 * q:32 * q + 4, :].bitcast(I32), w3_scales[0, 4 * q:4 * q + 4, :].bitcast(I32))
 
-        picked0 = gather_words(table0, "x_picked0", ((0, S),))
+        picked0 = gather_words(table0, "x_picked0", HALVES)
+        idle = psum.tile([P, 512], F32, name="idle", tag="acc", bufs=8)
+        for i in range(3):
+            nc.tensor.matmul_mx(out=idle[:], lhsT=picked0[:, 0:P].bitcast(FP8X4), lhsT_scale=scale_rows[:, 0:P],
+                                rhs=picked0[:, 0:512].bitcast(FP8X4), rhs_scale=scale_rows[:, 0:512], start=True, stop=True)
         qa = quantise_chunk(raw_a0, "wa0")
         picked1 = gather_words(table1, "x_picked1", TAPERED[0:1])
         qa = qa + quantise_chunk(raw_a1, "wa1")

@@ -96,11 +96,13 @@ def tile_picked_edgecv_relu_p_kernel(tc, x_words, x_scales, w1, w2, w3_words, w3
             for c0, c1 in pieces:
                 acc = psum.tile([P, c1 - c0], F32, name="acc", tag="acc", bufs=8)
                 for z in range(PASSES):
-                    words = picked0[:, c0:c1] if z == 0 else picked1[:] if c0 == 0 else picked2[:, c0 - 512:c1 - 512]
-                    nc.tensor.matmul_mx(
-                        out=acc[:], lhsT=weights[z][0].bitcast(FP8X4), lhsT_scale=weights[z][1],
-                        rhs=words.bitcast(FP8X4), rhs_scale=picked_scales[4 * z:P, c0:c1],
-                        start=(z == 0), stop=(z == PASSES - 1))
+                    for b0, b1, words in picked[z]:
+                        u0, u1 = max(b0, c0), min(b1, c1)
+                        if u0 < u1:
+                            nc.tensor.matmul_mx(
+                                out=acc[:, u0 - c0:u1 - c0], lhsT=weights[z][0].bitcast(FP8X4), lhsT_scale=weights[z][1],
+                                rhs=words[:, u0 - b0:u1 - b0].bitcast(FP8X4), rhs_scale=picked_scales[4 * z:P, u0:u1],
+                                start=(z == 0), stop=(z == PASSES - 1 and u1 == c1))
                 (last_copy if c0 >= 512 else nc.scalar.copy)(rows[:, c0:c1], acc[:])
             return rows
 
@@ -111,11 +113,11 @@ def tile_picked_edgecv_relu_p_kernel(tc, x_words, x_scales, w1, w2, w3_words, w3
             (nc.scalar, nc.sync)[z].dma_start(x_scale_table[z:32:2, 0:T].bitcast(I32), x_scales[z].bitcast(I32))
         offs_sb = load_list(offs, "offs_sb")
         table0 = load_words(0)
-        raw_a0 = load_weight(w2, 0, 0, 128, "raw_a0")
         pos1_sb = load_list(pos1, "pos1_sb")
         pos2_sb = load_list(pos2, "pos2_sb")
         cen_sb = load_list(cen, "cen_sb")
         table1 = load_words(1)
+        raw_a0 = load_weight(w2, 0, 0, 128, "raw_a0")
         raw_a1 = load_weight(w2, 1, 0, 128, "raw_a1")
 
         scale_rows = sb([P, S], U8, "scale_rows")
@@ -140,10 +142,12 @@ def tile_picked_edgecv_relu_p_kernel(tc, x_words, x_scales, w1, w2, w3_words, w3
         for i in range(3):
             nc.tensor.matmul_mx(out=idle[:], lhsT=picked0[:, 0:P].bitcast(FP8X4), lhsT_scale=scale_rows[:, 0:P],
                                 rhs=picked0[:, 0:512].bitcast(FP8X4), rhs_scale=scale_rows[:, 0:512], start=True, stop=True)
-        qa = quantise_chunk(raw_a0, "wa0")
         picked1 = gather_words(table1, "x_picked1", TAPERED[0:1])
+        qa = quantise_chunk(raw_a0, "wa0")
+        picked2 = gather_words(table1, "x_picked2", TAPERED[1:2], tag="raw_a0")
         qa = qa + quantise_chunk(raw_a1, "wa1")
-        picked2 = gather_words(table1, "x_picked2", TAPERED[1:3], tag="raw_a1")
+        picked3 = gather_words(table1, "x_picked3", TAPERED[2:3], tag="raw_a1")
+        picked = [[(0, S, picked0)], [(0, 512, picked1), (512, 768, picked2), (768, S, picked3)]]
         qb = quantise_chunk(raw_b[0], "wb0", "x_table1")
 
         edge = sb([P, PACK, V], F32, "edge")
@@ -171,9 +175,9 @@ def tile_picked_edgecv_relu_p_kernel(tc, x_words, x_scales, w1, w2, w3_words, w3
                             nc.sync.dma_start(m_half[i][t0 + u][rows, :], tile[u:P:P // run, 256 * i:256 * i + 256])
 
         e0 = product([qa[0], qa[1]], "e0", TAPERED, nc.vector.tensor_copy)
+        first0 = fetch(e0, pos1_sb, "first0")
         qb = qb + quantise_chunk(raw_b[1], "wb1")
-        first0 = fetch(e0, pos1_sb, "first0", 3)
-        second0 = fetch(e0, pos2_sb, "second0", 1)
+        second0 = fetch(e0, pos2_sb, "second0", 3)
         qc = quantise_chunk(raw_c[0], "wc0")
         larger(first0, second0, 0, 128, 0, kib=33)
         qc = qc + quantise_chunk(raw_c[1], "wc1")

@@ -41,7 +41,7 @@ def tile_picked_edgecv_relu_p_kernel(tc, x_words, x_scales, w1, w2, w3_words, w3
             return tile
 
         def load_words(z):
-            tile = sb([P, T], I32, "x_table%d" % (z,))
+            tile = placed([P, T], I32, "x_table%d" % (z,), (44, 36)[z])
             nc.sync.dma_start(tile[:, 0:T], x_words[z].rearrange("p c r -> p (c r)").bitcast(I32))
             return tile
 
@@ -53,36 +53,22 @@ def tile_picked_edgecv_relu_p_kernel(tc, x_words, x_scales, w1, w2, w3_words, w3
         def scalar_cast(dst, src):
             nc.scalar.activation(dst, src, ACT.Copy)
 
-        def gpsimd_cast(dst, src):
-            nc.gpsimd.tensor_scalar(dst, src, 1.0, 0.0, ALU.mult, ALU.add)
-
-        def quantise_weight(raws, name, codes_tag=None, shared=False, grouped_tag=None, kib=None):
-            width = raws[0].shape[2]
-            shape = [P, len(raws), PACK, width // PACK, PACK]
-            grouped = sb(shape, BF16, name + "_grouped", tag=grouped_tag) if kib is None else placed(shape, BF16, name + "_grouped", kib)
-            for z, raw in enumerate(raws):
-                if shared:
-                    gpsimd_cast(grouped[:, z, 0], raw[:].rearrange("p j (m t) -> p t m j", t=PACK)[:, 0])
-                    scalar_cast(grouped[:, z, 1:4].rearrange("p t m j -> p m j t"), raw[:].rearrange("p j (m t) -> p m j t", t=PACK)[:, :, :, 1:4])
-                else:
-                    scalar_cast(grouped[:, z].rearrange("p t m j -> p m j t"), raw[:].rearrange("p j (m t) -> p m j t", t=PACK))
-            codes = sb([P, len(raws) * width], U32, name + "_codes", tag=codes_tag)
-            scales = sb([P, len(raws) * width], U8, name + "_scales")
-            nc.vector.quantize_mx(out=codes[:].bitcast(FP8X4), scales=scales[:], in_=grouped[:].rearrange("p z t m j -> p (z t m j)"))
-            return [(codes[:, i:i + P], scales[:, i:i + P]) for i in range(0, len(raws) * width, P)]
-
-        def quantise_chunk(raw, name, codes_tag=None):
-            width = raw.shape[2]
-            tiles = width // P
-            grouped = sb([P, width, PACK], BF16, name + "_grouped")
-            if tiles == 1:
-                scalar_cast(grouped[:].rearrange("p (m t) j -> p m j t", t=PACK), raw[:].rearrange("p j (m t) -> p m j t", t=PACK))
-            else:
-                nc.scalar.copy(grouped[:].rearrange("p (u m e) j -> p m j u e", u=2, e=2), raw[:].rearrange("p j (m u e) -> p m j u e", u=2, e=2))
-            codes = sb([P, width], U32, name + "_codes", tag=codes_tag)
+        def quantise(grouped, name, kib=None):
+            width = grouped.shape[1] // PACK
+            codes = sb([P, width], U32, name + "_codes") if kib is None else placed([P, width], U32, name + "_codes", kib)
             scales = sb([P, width], U8, name + "_scales")
-            nc.vector.quantize_mx(out=codes[:].bitcast(FP8X4), scales=scales[:], in_=grouped[:].rearrange("p c j -> p (c j)"))
+            nc.vector.quantize_mx(out=codes[:].bitcast(FP8X4), scales=scales[:], in_=grouped)
             return [(codes[:, i:i + P], scales[:, i:i + P]) for i in range(0, width, P)]
+
+        def quantise_chunk(raw, name, kib=None):
+            grouped = sb([P, P, PACK], BF16, name + "_grouped")
+            scalar_cast(grouped[:].rearrange("p (m t) j -> p m j t", t=PACK), raw[:].rearrange("p j (m t) -> p m j t", t=PACK))
+            return quantise(grouped[:].rearrange("p c j -> p (c j)"), name, kib)
+
+        def cast_dealt(raw, t0, t1, name, kib):
+            grouped = placed([P, t1 - t0, P, PACK], BF16, name + "_grouped", kib)
+            nc.vector.tensor_copy(grouped[:].rearrange("p t m j -> p m j t"), raw[:].rearrange("p j (m t) -> p m j t", t=PACK)[:, :, :, t0:t1])
+            return grouped[:].rearrange("p t m j -> p (t m j)")
 
         def gather_words(table, name, pieces, tag=None):
             base = pieces[0][0]
@@ -106,7 +92,7 @@ def tile_picked_edgecv_relu_p_kernel(tc, x_words, x_scales, w1, w2, w3_words, w3
                 (last_copy if c0 >= 512 else nc.scalar.copy)(rows[:, c0:c1], acc[:])
             return rows
 
-        x_scale_table = placed([P, 50 * 1024], U8, "x_scale_table", 0)
+        x_scale_table = placed([P, 33 * 1024], U8, "x_scale_table", 0)
         nc.vector.memset(x_scale_table[32:64, 0:T].bitcast(I32), 0)
         nc.vector.memset(x_scale_table[64:P, 0:T].bitcast(I32), 0)
         for z in range(PASSES):
@@ -127,12 +113,12 @@ def tile_picked_edgecv_relu_p_kernel(tc, x_words, x_scales, w1, w2, w3_words, w3
             nc.sync.dma_start(picked_scales[r:P:4, :].bitcast(I32), scale_rows[2 * r:2 * r + 32, :].bitcast(I32))
 
         raw_b = [load_weight(w2, z, 128, 256, "raw_b%d" % z, 2 * z) for z in range(PASSES)]
-        raw_c = [load_weight(w2, z, 256, H, "raw_c%d" % z, (34, 44)[z]) for z in range(PASSES)]
-        raw10 = load_weight(w1, 0, 0, H, "raw10", 14)
-        raw11 = load_weight(w1, 1, 0, H, "raw11", 22)
-        w3_code = placed([P, N], U32, "w3_code", 30)
+        raw_c = [load_weight(w2, z, 256, H, "raw_c%d" % z, (6, 10)[z]) for z in range(PASSES)]
+        raw10 = load_weight(w1, 0, 0, H, "raw10", 16)
+        raw11 = load_weight(w1, 1, 0, H, "raw11", 24)
+        w3_code = placed([P, N], U32, "w3_code", 32)
         nc.sync.dma_start(w3_code[:].bitcast(I32), w3_words[0].rearrange("p c r -> p (c r)").bitcast(I32))
-        w3_scale = placed([P, N], U8, "w3_scale", 30.5)
+        w3_scale = placed([P, N], U8, "w3_scale", 32.5)
         nc.vector.memset(w3_scale[:].bitcast(I32), 0)
         for q in range(4):
             nc.sync.dma_start(w3_scale[32 * q:32 * q + 4, :].bitcast(I32), w3_scales[0, 4 * q:4 * q + 4, :].bitcast(I32))
@@ -148,89 +134,102 @@ def tile_picked_edgecv_relu_p_kernel(tc, x_words, x_scales, w1, w2, w3_words, w3
         qa = qa + quantise_chunk(raw_a1, "wa1")
         picked3 = gather_words(table1, "x_picked3", TAPERED[2:3], tag="raw_a1")
         picked = [[(0, S, picked0)], [(0, 512, picked1), (512, 768, picked2), (768, S, picked3)]]
-        qb = quantise_chunk(raw_b[0], "wb0", "x_table1")
+        qb = quantise_chunk(raw_b[0], "wb0", 36)
 
         edge = sb([P, PACK, V], F32, "edge")
-        m_full = [sb([P, V], F32, "larger%d" % (t,)) for t in range(4)]
-        m_half = [[m_full[t][:, 256 * i:256 * i + 256] if (i, t) != (0, 3) else edge[:, 2, 256:512] for t in range(4)] for i in range(2)]
+        m = [sb([P, V], F32, "larger%d" % (t,)) for t in range(4)]
 
-        def fetch(e_rows, places, name, kib=None, step=V):
+        def fetch(engine, rows, places, name, kib=None):
             tile = sb([P, V], F32, name) if kib is None else placed([P, V], F32, name, kib)
-            for v0 in range(0, V, step):
-                nc.vector.tensor_copy(tile[:, v0:v0 + step], e_rows[:].indirect(places[:, v0 // 16:(v0 + step) // 16]))
+            if engine == "vector":
+                nc.vector.tensor_copy(tile[:], rows[:].indirect(places[:]))
+            else:
+                nc.scalar.activation(tile[:], rows[:].indirect(places[:]), ACT.Copy)
             return tile
 
-        def larger(first, second, c0, width, t0, kib=None, step=V):
+        def larger(first, second, c0, width, t0, kib=None):
             name = "unplaced%d_%d" % (c0, t0)
             tile = sb([P, V], F32, name) if kib is None else placed([P, V], F32, name, kib)
             run = width // PACK
             rows = slice(c0 // PACK, c0 // PACK + run)
-            for v0 in range(0, V, step):
-                nc.vector.tensor_tensor(tile[:, v0:v0 + step], first[:, v0:v0 + step], second[:, v0:v0 + step], ALU.max)
-                for u in range(P // run):
-                    if step == V and t0 + u < 3:
-                        nc.sync.dma_start(m_full[t0 + u][rows, :], tile[u:P:P // run, :])
-                    else:
-                        for i in range(v0 // 256, (v0 + step) // 256):
-                            nc.sync.dma_start(m_half[i][t0 + u][rows, :], tile[u:P:P // run, 256 * i:256 * i + 256])
-
-        e0 = product([qa[0], qa[1]], "e0", TAPERED, nc.vector.tensor_copy)
-        first0 = fetch(e0, pos1_sb, "first0")
-        qb = qb + quantise_chunk(raw_b[1], "wb1")
-        second0 = fetch(e0, pos2_sb, "second0", 3)
-        qc = quantise_chunk(raw_c[0], "wc0")
-        larger(first0, second0, 0, 128, 0, kib=33)
-        qc = qc + quantise_chunk(raw_c[1], "wc1")
-        e1 = product(qb, "e1", kib=47)
-        first1 = fetch(e1, pos1_sb, "first1")
-        second1 = fetch(e1, pos2_sb, "second1")
-        e2 = product([qc[0], qc[2]], "e2", kib=14)
-        q10 = quantise_weight([raw10], "w10", shared=True, grouped_tag="wc1_grouped")
-        larger(first1, second1, 128, 128, 0, kib=18)
-        first2 = fetch(e2, pos1_sb, "first2")
-        second2 = fetch(e2, pos2_sb, "second2")
-        e3 = product([qc[1], qc[3]], "e3", kib=22)
-        q11 = quantise_weight([raw11], "w11", shared=True, grouped_tag="wc1_grouped")
-        larger(first2, second2, 256, 256, 0, kib=26)
-        first3 = fetch(e3, pos1_sb, "first3")
-        second3 = fetch(e3, pos2_sb, "second3", step=256)
-        larger(first3, second3, 256, 256, 2, step=256)
-        y = [product([q10[t], q11[t]], "y%d" % (t,)) for t in range(4)]
+            nc.vector.tensor_tensor(tile[:], first[:], second[:], ALU.max)
+            for u in range(P // run):
+                nc.sync.dma_start(m[t0 + u][rows, :], tile[u:P:P // run, :])
 
         def add_centres(v0, v1, t):
-            larger_part = m_half[v0 // 256][t][:, v0 % 256:v0 % 256 + v1 - v0]
-            nc.vector.tensor_tensor(edge[:, t, v0:v1], y[t][:].indirect(cen_sb[:, v0 // 16:v1 // 16]), larger_part, ALU.add)
+            nc.vector.tensor_tensor(edge[:, t, v0:v1], y[t][:].indirect(cen_sb[:, v0 // 16:v1 // 16]), m[t][:, v0:v1], ALU.add)
 
-        def scalar_relu(dst, src):
-            nc.scalar.activation(dst, src, ACT.Relu)
+        gb = placed([P, P, PACK], BF16, "wb1_grouped", 38)
+        nc.vector.tensor_copy(gb[:].rearrange("p (m t) j -> p m j t", t=PACK), raw_b[1][:].rearrange("p j (m t) -> p m j t", t=PACK))
+        e0 = product([qa[0], qa[1]], "e0", TAPERED)
+        qb = qb + quantise(gb[:].rearrange("p c j -> p (c j)"), "wb1", 39)
 
-        def vector_relu(dst, src):
-            nc.vector.tensor_scalar_max(dst, src, 0.0)
+        def cast_paired(z, kib):
+            grouped = placed([P, 256, PACK], BF16, "wc%d_grouped" % z, kib)
+            nc.vector.tensor_copy(grouped[:].rearrange("p (u m e) j -> p m j u e", u=2, e=2), raw_c[z][:].rearrange("p j (m u e) -> p m j u e", u=2, e=2))
+            return grouped[:].rearrange("p c j -> p (c j)")
 
-        res_sb = sb([P, V], F32, "res_sb")
+        first0 = fetch("vector", e0, pos1_sb, "first0", 4)
+        second0 = fetch("scalar", e0, pos2_sb, "second0")
+        gc0 = cast_paired(0, 37.75)
+        larger(first0, second0, 0, 128, 0)
+        qc = quantise(gc0, "wc0")
+        qc = qc + quantise(cast_paired(1, 5), "wc1")
+        e1 = product(qb, "e1")
+        second1 = fetch("scalar", e1, pos2_sb, "second1")
+        first1 = fetch("scalar", e1, pos1_sb, "first1")
+        g10 = cast_dealt(raw10, 0, 4, "w10", 6.5)
+        larger(first1, second1, 128, 128, 0, kib=19.5)
+        q10 = quantise(g10, "w10")
+        e2 = product([qc[0], qc[2]], "e2")
+        second2 = fetch("scalar", e2, pos2_sb, "second2")
+        first2 = fetch("vector", e2, pos1_sb, "first2", 22)
+        g11a = cast_dealt(raw11, 0, 2, "w11a", 5.5)
+        larger(first2, second2, 256, 256, 0)
+        q11 = quantise(g11a, "w11a")
+        e3 = product([qc[1], qc[3]], "e3")
+        second3 = fetch("scalar", e3, pos2_sb, "second3")
+        first3 = sb([P, V], F32, "first3")
+        nc.vector.tensor_copy(first3[:, 0:256], e3[:].indirect(pos1_sb[:, 0:16]))
+        nc.scalar.activation(first3[:, 256:V], e3[:].indirect(pos1_sb[:, 16:32]), ACT.Copy)
+        g11b = cast_dealt(raw11, 2, 4, "w11b", 5.5)
+        larger(first3, second3, 256, 256, 2)
+        q11 = q11 + quantise(g11b, "w11b")
+        y = [product([q10[t], q11[t]], "y%d" % (t,)) for t in range(4)]
+        add_centres(0, V, 0)
 
-        def project(v0, v1, relu, copy=nc.scalar.copy):
-            n = v1 - v0
-            z = sb([P, n, PACK], BF16, "z%d" % v0)
-            for u0 in range(0, n, 128):
-                sums = edge[:, :, v0 + u0:min(v0 + u0 + 128, v1)]
-                relu(z[:, u0:min(u0 + 128, n)].rearrange("p (c i) t -> p c t i", i=4), sums.rearrange("p t (c i) -> p c t i", i=4))
-            z_codes = sb([P, n], U32, "z_codes%d" % v0)
-            z_scales = sb([P, n], U8, "z_scales%d" % v0)
-            nc.vector.quantize_mx(out=z_codes[:].bitcast(FP8X4), scales=z_scales[:], in_=z[:].rearrange("p c t -> p (c t)"))
+        def relu_views(z, base, v0, v1):
+            return (z[:, v0 - base:v1 - base].rearrange("p (c i) t -> p c t i", i=4), edge[:, :, v0:v1].rearrange("p t (c i) -> p c t i", i=4))
+
+        def project(name, pieces, copy, res_sb):
+            n = sum(z.shape[1] for z in pieces)
+            z_codes = sb([P, n], U32, name + "_codes")
+            z_scales = sb([P, n], U8, name + "_scales")
+            c0 = 0
+            for z in pieces:
+                c1 = c0 + z.shape[1]
+                nc.vector.quantize_mx(out=z_codes[:, c0:c1].bitcast(FP8X4), scales=z_scales[:, c0:c1], in_=z[:].rearrange("p c t -> p (c t)"))
+                c0 = c1
             res = psum.tile([P, n], F32, name="res", tag="acc", bufs=8)
             nc.tensor.matmul_mx(out=res[:], lhsT=w3_code[:].bitcast(FP8X4), lhsT_scale=w3_scale[:],
                                 rhs=z_codes[:].bitcast(FP8X4), rhs_scale=z_scales[:], start=True, stop=True)
-            copy(res_sb[:, v0:v1], res[:])
+            copy(res_sb, res[:])
 
-        for t in range(2):
-            nc.vector.tensor_tensor(edge[:, t, :], y[t][:].indirect(cen_sb[:]), m_full[t][:], ALU.add)
-        for v0, v1, t in ((0, 256, 2), (0, 128, 3), (128, 256, 3), (256, 384, 2), (256, 384, 3), (384, 512, 2), (384, 448, 3), (448, 512, 3)):
+        for v0, v1, t in ((0, 512, 1), (0, 256, 2), (0, 128, 3), (128, 256, 3), (256, 384, 2), (256, 384, 3), (384, 512, 2), (384, 448, 3), (448, 512, 3)):
             add_centres(v0, v1, t)
-        project(0, 256, scalar_relu)
-        nc.sync.dma_start(out[:, 0:256], res_sb[:, 0:256])
-        project(256, 384, scalar_relu)
-        nc.sync.dma_start(out[:, 256:384], res_sb[:, 256:384])
-        project(384, 448, scalar_relu)
-        project(448, 512, vector_relu, nc.vector.tensor_copy)
-        nc.sync.dma_start(out[:, 384:V], res_sb[:, 384:V])
+        za = placed([P, 256, PACK], BF16, "za", 12)
+        zb = sb([P, 128, PACK], BF16, "zb")
+        zc = sb([P, 64, PACK], BF16, "zc")
+        for z, base, v0, v1 in ((za, 0, 0, 128), (za, 0, 128, 256), (zb, 256, 256, 384), (zc, 384, 384, 448)):
+            dst, src = relu_views(z, base, v0, v1)
+            nc.scalar.activation(dst, src, ACT.Relu)
+        res_a = sb([P, 256], F32, "res_a")
+        res_b = sb([P, 256], F32, "res_b")
+        project("za", [za], nc.scalar.copy, res_a[:])
+        nc.sync.dma_start(out[:, 0:256], res_a[:])
+        zd = placed([P, 64, PACK], BF16, "zd", 12)
+        dst, src = relu_views(zd, 448, 448, 512)
+        nc.vector.tensor_scalar_max(dst, src, 0.0)
+        project("zb", [zb], nc.scalar.copy, res_b[:, 0:128])
+        project("zc", [zc, zd], nc.vector.tensor_copy, res_b[:, 128:256])
+        nc.sync.dma_start(out[:, 256:V], res_b[:])

@@ -77,18 +77,18 @@ def tile_picked_edgecv_relu_p_kernel(tc, x_words, x_scales, w1, w2, w3_words, w3
                 nc.vector.tensor_copy(tile[:, c0 - base:c1 - base], table[:, 0:T].bitcast(U32).indirect(offs_sb[:, c0 // 16:c1 // 16]))
             return tile
 
-        def product(weights, name, pieces=HALVES, last_copy=nc.scalar.copy, kib=None):
+        def product(weights, name, pieces=HALVES, last_copy=nc.scalar.copy, kib=None, order=(0, 1)):
             rows = sb([P, S], F32, name) if kib is None else placed([P, S], F32, name, kib)
             for c0, c1 in pieces:
                 acc = psum.tile([P, c1 - c0], F32, name="acc", tag="acc", bufs=8)
-                for z in range(PASSES):
+                for z in order:
                     for b0, b1, words in picked[z]:
                         u0, u1 = max(b0, c0), min(b1, c1)
                         if u0 < u1:
                             nc.tensor.matmul_mx(
                                 out=acc[:, u0 - c0:u1 - c0], lhsT=weights[z][0].bitcast(FP8X4), lhsT_scale=weights[z][1],
                                 rhs=words[:, u0 - b0:u1 - b0].bitcast(FP8X4), rhs_scale=picked_scales[4 * z:P, u0:u1],
-                                start=(z == 0), stop=(z == PASSES - 1 and u1 == c1))
+                                start=(z == order[0] and u0 == c0), stop=(z == order[-1] and u1 == c1))
                 (last_copy if c0 >= 512 else nc.scalar.copy)(rows[:, c0:c1], acc[:])
             return rows
 
@@ -187,11 +187,9 @@ def tile_picked_edgecv_relu_p_kernel(tc, x_words, x_scales, w1, w2, w3_words, w3
         g11a = cast_dealt(raw11, 0, 2, "w11a", 5.5)
         larger(first2, second2, 256, 256, 0)
         q11 = quantise(g11a, "w11a")
-        e3 = product([qc[1], qc[3]], "e3")
+        e3 = product([qc[1], qc[3]], "e3", order=(1, 0))
         second3 = fetch("scalar", e3, pos2_sb, "second3")
-        first3 = sb([P, V], F32, "first3")
-        nc.vector.tensor_copy(first3[:, 0:256], e3[:].indirect(pos1_sb[:, 0:16]))
-        nc.scalar.activation(first3[:, 256:V], e3[:].indirect(pos1_sb[:, 16:32]), ACT.Copy)
+        first3 = fetch("vector", e3, pos1_sb, "first3")
         g11b = cast_dealt(raw11, 2, 4, "w11b", 5.5)
         larger(first3, second3, 256, 256, 2)
         q11 = q11 + quantise(g11b, "w11b")

@@ -18,22 +18,37 @@ ACT = mybir.ActivationFunctionType
 P = 128
 PACK = 4
 PASSES = K // (P * PACK)
+BANKS = 8
 HALVES = ((0, 512), (512, 1024))
 TAPERED = ((0, 512), (512, 768), (768, 1024))
+
+SCALE_TABLE_KIB = 33
+AT_RAW_B = (0, 2)
+AT_RAW_C = (6, 10)
+AT_RAW_W1 = (16, 24)
+AT_W3_WORDS, AT_W3_SCALES = 32, 32.5
+AT_WORD_TABLE = (44, 36)
+AT_CODES_B0, AT_CAST_B1, AT_CODES_B1 = 36, 38, 39
+AT_CAST_C0 = 37.75
+AT_FIRST0 = 4
+AT_CAST_C1 = 5
+AT_CAST_W10 = 6.5
+AT_LARGER1, AT_FIRST2 = 19.5, 22
+AT_CAST_W11 = 5.5
+AT_Z_FIRST_LAST = 12
 
 
 def tile_picked_edgecv_relu_p_kernel(tc, x_words, x_scales, w1, w2, w3_words, w3_scales, offs, cen, pos1, pos2, out):
     nc = tc.nc
     with ExitStack() as ctx:
         keep = ctx.enter_context(tc.tile_pool(name="keep", bufs=1))
-        late = ctx.enter_context(tc.tile_pool(name="late", bufs=1))
+        reused = ctx.enter_context(tc.tile_pool(name="reused", bufs=1))
         psum = ctx.enter_context(tc.psum_pool(name="psum", bufs=1))
 
-        def sb(shape, dtype, name, tag=None, bufs=1):
-            return keep.tile(shape, dtype, name=name, tag=tag or name, bufs=bufs, align_bytes=64)
-
-        def placed(shape, dtype, name, kib):
-            return late.tile(shape, dtype, name=name, align_bytes=64, offset=int(kib * 1024))
+        def sb(shape, dtype, name, kib=None, tag=None):
+            if kib is None:
+                return keep.tile(shape, dtype, name=name, tag=tag or name, bufs=1, align_bytes=64)
+            return reused.tile(shape, dtype, name=name, align_bytes=64, offset=int(kib * 1024))
 
         def load_list(src, name):
             tile = keep.tile(list(src.shape), U16, name=name)
@@ -41,46 +56,51 @@ def tile_picked_edgecv_relu_p_kernel(tc, x_words, x_scales, w1, w2, w3_words, w3
             return tile
 
         def load_words(z):
-            tile = placed([P, T], I32, "x_table%d" % (z,), (44, 36)[z])
-            nc.sync.dma_start(tile[:, 0:T], x_words[z].rearrange("p c r -> p (c r)").bitcast(I32))
+            tile = sb([P, T], I32, "x_table%d" % (z,), AT_WORD_TABLE[z])
+            nc.sync.dma_start(tile[:], x_words[z].rearrange("p c r -> p (c r)").bitcast(I32))
             return tile
 
         def load_weight(w, z, c0, c1, name, kib=None):
-            tile = sb([P, PACK, c1 - c0], F32, name) if kib is None else placed([P, PACK, c1 - c0], F32, name, kib)
+            tile = sb([P, PACK, c1 - c0], F32, name, kib)
             nc.sync.dma_start(tile[:], w[z * 512:(z + 1) * 512, c0:c1].rearrange("(p j) c -> p j c", j=PACK))
             return tile
 
         def scalar_cast(dst, src):
             nc.scalar.activation(dst, src, ACT.Copy)
 
+        def cast_plain(cast, raw, name, kib=None):
+            grouped = sb([P, P, PACK], BF16, name + "_grouped", kib)
+            cast(grouped[:].rearrange("p (m t) j -> p m j t", t=PACK), raw[:].rearrange("p j (m t) -> p m j t", t=PACK))
+            return grouped[:].rearrange("p c j -> p (c j)")
+
+        def cast_paired(raw, name, kib):
+            grouped = sb([P, 256, PACK], BF16, name + "_grouped", kib)
+            nc.vector.tensor_copy(grouped[:].rearrange("p (u m d) j -> p m j u d", u=2, d=2), raw[:].rearrange("p j (m u d) -> p m j u d", u=2, d=2))
+            return grouped[:].rearrange("p c j -> p (c j)")
+
+        def cast_dealt(raw, t0, t1, name, kib):
+            grouped = sb([P, t1 - t0, P, PACK], BF16, name + "_grouped", kib)
+            nc.vector.tensor_copy(grouped[:].rearrange("p t m j -> p m j t"), raw[:].rearrange("p j (m t) -> p m j t", t=PACK)[:, :, :, t0:t1])
+            return grouped[:].rearrange("p t m j -> p (t m j)")
+
         def quantise(grouped, name, kib=None):
             width = grouped.shape[1] // PACK
-            codes = sb([P, width], U32, name + "_codes") if kib is None else placed([P, width], U32, name + "_codes", kib)
+            codes = sb([P, width], U32, name + "_codes", kib)
             scales = sb([P, width], U8, name + "_scales")
             nc.vector.quantize_mx(out=codes[:].bitcast(FP8X4), scales=scales[:], in_=grouped)
             return [(codes[:, i:i + P], scales[:, i:i + P]) for i in range(0, width, P)]
-
-        def quantise_chunk(raw, name, kib=None):
-            grouped = sb([P, P, PACK], BF16, name + "_grouped")
-            scalar_cast(grouped[:].rearrange("p (m t) j -> p m j t", t=PACK), raw[:].rearrange("p j (m t) -> p m j t", t=PACK))
-            return quantise(grouped[:].rearrange("p c j -> p (c j)"), name, kib)
-
-        def cast_dealt(raw, t0, t1, name, kib):
-            grouped = placed([P, t1 - t0, P, PACK], BF16, name + "_grouped", kib)
-            nc.vector.tensor_copy(grouped[:].rearrange("p t m j -> p m j t"), raw[:].rearrange("p j (m t) -> p m j t", t=PACK)[:, :, :, t0:t1])
-            return grouped[:].rearrange("p t m j -> p (t m j)")
 
         def gather_words(table, name, pieces, tag=None):
             base = pieces[0][0]
             tile = sb([P, pieces[-1][1] - base], U32, name, tag=tag)
             for c0, c1 in pieces:
-                nc.vector.tensor_copy(tile[:, c0 - base:c1 - base], table[:, 0:T].bitcast(U32).indirect(offs_sb[:, c0 // 16:c1 // 16]))
+                nc.vector.tensor_copy(tile[:, c0 - base:c1 - base], table[:].bitcast(U32).indirect(offs_sb[:, c0 // 16:c1 // 16]))
             return tile
 
-        def product(weights, name, pieces=HALVES, last_copy=nc.scalar.copy, kib=None, order=(0, 1)):
-            rows = sb([P, S], F32, name) if kib is None else placed([P, S], F32, name, kib)
+        def product(weights, name, pieces=HALVES, order=(0, 1)):
+            rows = sb([P, S], F32, name)
             for c0, c1 in pieces:
-                acc = psum.tile([P, c1 - c0], F32, name="acc", tag="acc", bufs=8)
+                acc = psum.tile([P, c1 - c0], F32, name="acc", tag="acc", bufs=BANKS)
                 for z in order:
                     for b0, b1, words in picked[z]:
                         u0, u1 = max(b0, c0), min(b1, c1)
@@ -89,10 +109,10 @@ def tile_picked_edgecv_relu_p_kernel(tc, x_words, x_scales, w1, w2, w3_words, w3
                                 out=acc[:, u0 - c0:u1 - c0], lhsT=weights[z][0].bitcast(FP8X4), lhsT_scale=weights[z][1],
                                 rhs=words[:, u0 - b0:u1 - b0].bitcast(FP8X4), rhs_scale=picked_scales[4 * z:P, u0:u1],
                                 start=(z == order[0] and u0 == c0), stop=(z == order[-1] and u1 == c1))
-                (last_copy if c0 >= 512 else nc.scalar.copy)(rows[:, c0:c1], acc[:])
+                nc.scalar.copy(rows[:, c0:c1], acc[:])
             return rows
 
-        x_scale_table = placed([P, 33 * 1024], U8, "x_scale_table", 0)
+        x_scale_table = sb([P, SCALE_TABLE_KIB * 1024], U8, "x_scale_table", 0)
         nc.vector.memset(x_scale_table[32:64, 0:T].bitcast(I32), 0)
         nc.vector.memset(x_scale_table[64:P, 0:T].bitcast(I32), 0)
         for z in range(PASSES):
@@ -103,8 +123,7 @@ def tile_picked_edgecv_relu_p_kernel(tc, x_words, x_scales, w1, w2, w3_words, w3
         pos2_sb = load_list(pos2, "pos2_sb")
         cen_sb = load_list(cen, "cen_sb")
         table1 = load_words(1)
-        raw_a0 = load_weight(w2, 0, 0, 128, "raw_a0")
-        raw_a1 = load_weight(w2, 1, 0, 128, "raw_a1")
+        raw_a = [load_weight(w2, z, 0, 128, "raw_a%d" % z) for z in range(PASSES)]
 
         scale_rows = sb([P, S], U8, "scale_rows")
         nc.vector.tensor_copy(scale_rows[:], x_scale_table[:, 0:T].indirect(offs_sb[:]))
@@ -112,120 +131,113 @@ def tile_picked_edgecv_relu_p_kernel(tc, x_words, x_scales, w1, w2, w3_words, w3
         for r in range(4):
             nc.sync.dma_start(picked_scales[r:P:4, :].bitcast(I32), scale_rows[2 * r:2 * r + 32, :].bitcast(I32))
 
-        raw_b = [load_weight(w2, z, 128, 256, "raw_b%d" % z, 2 * z) for z in range(PASSES)]
-        raw_c = [load_weight(w2, z, 256, H, "raw_c%d" % z, (6, 10)[z]) for z in range(PASSES)]
-        raw10 = load_weight(w1, 0, 0, H, "raw10", 16)
-        raw11 = load_weight(w1, 1, 0, H, "raw11", 24)
-        w3_code = placed([P, N], U32, "w3_code", 32)
+        raw_b = [load_weight(w2, z, 128, 256, "raw_b%d" % z, AT_RAW_B[z]) for z in range(PASSES)]
+        raw_c = [load_weight(w2, z, 256, H, "raw_c%d" % z, AT_RAW_C[z]) for z in range(PASSES)]
+        raw_w1 = [load_weight(w1, z, 0, H, "raw_w1%d" % z, AT_RAW_W1[z]) for z in range(PASSES)]
+        w3_code = sb([P, N], U32, "w3_code", AT_W3_WORDS)
         nc.sync.dma_start(w3_code[:].bitcast(I32), w3_words[0].rearrange("p c r -> p (c r)").bitcast(I32))
-        w3_scale = placed([P, N], U8, "w3_scale", 32.5)
+        w3_scale = sb([P, N], U8, "w3_scale", AT_W3_SCALES)
         nc.vector.memset(w3_scale[:].bitcast(I32), 0)
         for q in range(4):
             nc.sync.dma_start(w3_scale[32 * q:32 * q + 4, :].bitcast(I32), w3_scales[0, 4 * q:4 * q + 4, :].bitcast(I32))
 
         picked0 = gather_words(table0, "x_picked0", HALVES)
-        idle = psum.tile([P, 512], F32, name="idle", tag="acc", bufs=8)
-        for i in range(3):
-            nc.tensor.matmul_mx(out=idle[:], lhsT=picked0[:, 0:P].bitcast(FP8X4), lhsT_scale=scale_rows[:, 0:P],
-                                rhs=picked0[:, 0:512].bitcast(FP8X4), rhs_scale=scale_rows[:, 0:512], start=True, stop=True)
         picked1 = gather_words(table1, "x_picked1", TAPERED[0:1])
-        qa = quantise_chunk(raw_a0, "wa0")
+        qa = quantise(cast_plain(scalar_cast, raw_a[0], "wa0"), "wa0")
         picked2 = gather_words(table1, "x_picked2", TAPERED[1:2], tag="raw_a0")
-        qa = qa + quantise_chunk(raw_a1, "wa1")
+        qa = qa + quantise(cast_plain(scalar_cast, raw_a[1], "wa1"), "wa1")
         picked3 = gather_words(table1, "x_picked3", TAPERED[2:3], tag="raw_a1")
         picked = [[(0, S, picked0)], [(0, 512, picked1), (512, 768, picked2), (768, S, picked3)]]
-        qb = quantise_chunk(raw_b[0], "wb0", 36)
+        qb = quantise(cast_plain(scalar_cast, raw_b[0], "wb0"), "wb0", AT_CODES_B0)
 
         edge = sb([P, PACK, V], F32, "edge")
-        m = [sb([P, V], F32, "larger%d" % (t,)) for t in range(4)]
+        dealt = [sb([P, V], F32, "larger%d" % (t,)) for t in range(PACK)]
 
-        def fetch(engine, rows, places, name, kib=None):
-            tile = sb([P, V], F32, name) if kib is None else placed([P, V], F32, name, kib)
-            if engine == "vector":
-                nc.vector.tensor_copy(tile[:], rows[:].indirect(places[:]))
-            else:
-                nc.scalar.activation(tile[:], rows[:].indirect(places[:]), ACT.Copy)
+        def vector_fetch(rows, places, name, kib=None):
+            tile = sb([P, V], F32, name, kib)
+            nc.vector.tensor_copy(tile[:], rows[:].indirect(places[:]))
+            return tile
+
+        def scalar_fetch(rows, places, name):
+            tile = sb([P, V], F32, name)
+            nc.scalar.activation(tile[:], rows[:].indirect(places[:]), ACT.Copy)
             return tile
 
         def larger(first, second, c0, width, t0, kib=None):
-            name = "unplaced%d_%d" % (c0, t0)
-            tile = sb([P, V], F32, name) if kib is None else placed([P, V], F32, name, kib)
+            tile = sb([P, V], F32, "unplaced%d_%d" % (c0, t0), kib)
             run = width // PACK
             rows = slice(c0 // PACK, c0 // PACK + run)
             nc.vector.tensor_tensor(tile[:], first[:], second[:], ALU.max)
             for u in range(P // run):
-                nc.sync.dma_start(m[t0 + u][rows, :], tile[u:P:P // run, :])
+                nc.sync.dma_start(dealt[t0 + u][rows, :], tile[u:P:P // run, :])
 
         def add_centres(v0, v1, t):
-            nc.vector.tensor_tensor(edge[:, t, v0:v1], y[t][:].indirect(cen_sb[:, v0 // 16:v1 // 16]), m[t][:, v0:v1], ALU.add)
+            nc.vector.tensor_tensor(edge[:, t, v0:v1], y[t][:].indirect(cen_sb[:, v0 // 16:v1 // 16]), dealt[t][:, v0:v1], ALU.add)
 
-        gb = placed([P, P, PACK], BF16, "wb1_grouped", 38)
-        nc.vector.tensor_copy(gb[:].rearrange("p (m t) j -> p m j t", t=PACK), raw_b[1][:].rearrange("p j (m t) -> p m j t", t=PACK))
-        e0 = product([qa[0], qa[1]], "e0", TAPERED)
-        qb = qb + quantise(gb[:].rearrange("p c j -> p (c j)"), "wb1", 39)
-
-        def cast_paired(z, kib):
-            grouped = placed([P, 256, PACK], BF16, "wc%d_grouped" % z, kib)
-            nc.vector.tensor_copy(grouped[:].rearrange("p (u m e) j -> p m j u e", u=2, e=2), raw_c[z][:].rearrange("p j (m u e) -> p m j u e", u=2, e=2))
-            return grouped[:].rearrange("p c j -> p (c j)")
-
-        first0 = fetch("vector", e0, pos1_sb, "first0", 4)
-        second0 = fetch("scalar", e0, pos2_sb, "second0")
-        gc0 = cast_paired(0, 37.75)
+        cast_b1 = cast_plain(nc.vector.tensor_copy, raw_b[1], "wb1", AT_CAST_B1)
+        e0 = product(qa, "e0", TAPERED)
+        qb = qb + quantise(cast_b1, "wb1", AT_CODES_B1)
+        first0 = vector_fetch(e0, pos1_sb, "first0", AT_FIRST0)
+        second0 = scalar_fetch(e0, pos2_sb, "second0")
+        cast_c0 = cast_paired(raw_c[0], "wc0", AT_CAST_C0)
         larger(first0, second0, 0, 128, 0)
-        qc = quantise(gc0, "wc0")
-        qc = qc + quantise(cast_paired(1, 5), "wc1")
+        qc = quantise(cast_c0, "wc0")
+        qc = qc + quantise(cast_paired(raw_c[1], "wc1", AT_CAST_C1), "wc1")
         e1 = product(qb, "e1")
-        second1 = fetch("scalar", e1, pos2_sb, "second1")
-        first1 = fetch("scalar", e1, pos1_sb, "first1")
-        g10 = cast_dealt(raw10, 0, 4, "w10", 6.5)
-        larger(first1, second1, 128, 128, 0, kib=19.5)
-        q10 = quantise(g10, "w10")
+        second1 = scalar_fetch(e1, pos2_sb, "second1")
+        first1 = scalar_fetch(e1, pos1_sb, "first1")
+        cast_w10 = cast_dealt(raw_w1[0], 0, 4, "w10", AT_CAST_W10)
+        larger(first1, second1, 128, 128, 0, AT_LARGER1)
+        q10 = quantise(cast_w10, "w10")
         e2 = product([qc[0], qc[2]], "e2")
-        second2 = fetch("scalar", e2, pos2_sb, "second2")
-        first2 = fetch("vector", e2, pos1_sb, "first2", 22)
-        g11a = cast_dealt(raw11, 0, 2, "w11a", 5.5)
+        second2 = scalar_fetch(e2, pos2_sb, "second2")
+        first2 = vector_fetch(e2, pos1_sb, "first2", AT_FIRST2)
+        cast_w11 = cast_dealt(raw_w1[1], 0, 2, "w11a", AT_CAST_W11)
         larger(first2, second2, 256, 256, 0)
-        q11 = quantise(g11a, "w11a")
+        q11 = quantise(cast_w11, "w11a")
         e3 = product([qc[1], qc[3]], "e3", order=(1, 0))
-        second3 = fetch("scalar", e3, pos2_sb, "second3")
-        first3 = fetch("vector", e3, pos1_sb, "first3")
-        g11b = cast_dealt(raw11, 2, 4, "w11b", 5.5)
+        second3 = scalar_fetch(e3, pos2_sb, "second3")
+        first3 = vector_fetch(e3, pos1_sb, "first3")
+        cast_w11 = cast_dealt(raw_w1[1], 2, 4, "w11b", AT_CAST_W11)
         larger(first3, second3, 256, 256, 2)
-        q11 = q11 + quantise(g11b, "w11b")
-        y = [product([q10[t], q11[t]], "y%d" % (t,)) for t in range(4)]
-        add_centres(0, V, 0)
+        q11 = q11 + quantise(cast_w11, "w11b")
+        y = [product([q10[t], q11[t]], "y%d" % (t,)) for t in range(PACK)]
 
-        def relu_views(z, base, v0, v1):
-            return (z[:, v0 - base:v1 - base].rearrange("p (c i) t -> p c t i", i=4), edge[:, :, v0:v1].rearrange("p t (c i) -> p c t i", i=4))
+        def relu_views(z_tile, base, v0, v1):
+            return (z_tile[:, v0 - base:v1 - base].rearrange("p (c i) t -> p c t i", i=4), edge[:, :, v0:v1].rearrange("p t (c i) -> p c t i", i=4))
 
-        def project(name, pieces, copy, res_sb):
-            n = sum(z.shape[1] for z in pieces)
+        def project(name, z_tiles, copy, res_sb):
+            n = sum(z_tile.shape[1] for z_tile in z_tiles)
             z_codes = sb([P, n], U32, name + "_codes")
             z_scales = sb([P, n], U8, name + "_scales")
             c0 = 0
-            for z in pieces:
-                c1 = c0 + z.shape[1]
-                nc.vector.quantize_mx(out=z_codes[:, c0:c1].bitcast(FP8X4), scales=z_scales[:, c0:c1], in_=z[:].rearrange("p c t -> p (c t)"))
+            for z_tile in z_tiles:
+                c1 = c0 + z_tile.shape[1]
+                nc.vector.quantize_mx(out=z_codes[:, c0:c1].bitcast(FP8X4), scales=z_scales[:, c0:c1], in_=z_tile[:].rearrange("p c t -> p (c t)"))
                 c0 = c1
-            res = psum.tile([P, n], F32, name="res", tag="acc", bufs=8)
+            res = psum.tile([P, n], F32, name="res", tag="acc", bufs=BANKS)
             nc.tensor.matmul_mx(out=res[:], lhsT=w3_code[:].bitcast(FP8X4), lhsT_scale=w3_scale[:],
                                 rhs=z_codes[:].bitcast(FP8X4), rhs_scale=z_scales[:], start=True, stop=True)
             copy(res_sb, res[:])
 
-        for v0, v1, t in ((0, 512, 1), (0, 256, 2), (0, 128, 3), (128, 256, 3), (256, 384, 2), (256, 384, 3), (384, 512, 2), (384, 448, 3), (448, 512, 3)):
-            add_centres(v0, v1, t)
-        za = placed([P, 256, PACK], BF16, "za", 12)
+        for t in (0, 1):
+            add_centres(0, V, t)
+        for v0, v1, pieces in ((0, 256, 2), (256, 384, 1), (384, 512, 2)):
+            add_centres(v0, v1, 2)
+            step = (v1 - v0) // pieces
+            for u0 in range(v0, v1, step):
+                add_centres(u0, u0 + step, 3)
+        za = sb([P, 256, PACK], BF16, "za", AT_Z_FIRST_LAST)
         zb = sb([P, 128, PACK], BF16, "zb")
         zc = sb([P, 64, PACK], BF16, "zc")
-        for z, base, v0, v1 in ((za, 0, 0, 128), (za, 0, 128, 256), (zb, 256, 256, 384), (zc, 384, 384, 448)):
-            dst, src = relu_views(z, base, v0, v1)
+        for z_tile, base, v0, v1 in ((za, 0, 0, 128), (za, 0, 128, 256), (zb, 256, 256, 384), (zc, 384, 384, 448)):
+            dst, src = relu_views(z_tile, base, v0, v1)
             nc.scalar.activation(dst, src, ACT.Relu)
         res_a = sb([P, 256], F32, "res_a")
         res_b = sb([P, 256], F32, "res_b")
         project("za", [za], nc.scalar.copy, res_a[:])
         nc.sync.dma_start(out[:, 0:256], res_a[:])
-        zd = placed([P, 64, PACK], BF16, "zd", 12)
+        zd = sb([P, 64, PACK], BF16, "zd", AT_Z_FIRST_LAST)
         dst, src = relu_views(zd, 448, 448, 512)
         nc.vector.tensor_scalar_max(dst, src, 0.0)
         project("zb", [zb], nc.scalar.copy, res_b[:, 0:128])

from contextlib import ExitStack

import concourse.mybir as mybir

K, T, S, V, H, N = 1024, 2048, 1024, 512, 512, 128
FLOPS = 2 * (2 * K * H * S + H * N * V)

F32 = mybir.dt.float32
BF16 = mybir.dt.bfloat16
I32 = mybir.dt.int32
U32 = mybir.dt.uint32
U16 = mybir.dt.uint16
U8 = mybir.dt.uint8
FP8X4 = mybir.dt.float8_e4m3fn_x4
ALU = mybir.AluOpType
ACT = mybir.ActivationFunctionType

P = 128
PACK = 4
PASSES = K // (P * PACK)
BANKS = 8
HALVES = ((0, 512), (512, 1024))
TAPERED = ((0, 512), (512, 768), (768, 1024))

SCALE_TABLE_KIB = 33
AT_RAW_B = (0, 2)
AT_RAW_C = (6, 10)
AT_RAW_W1 = (16, 24)
AT_W3_WORDS, AT_W3_SCALES = 32, 32.5
AT_WORD_TABLE = (44, 36)
AT_CODES_B0, AT_CAST_B1, AT_CODES_B1 = 36, 38, 39
AT_CAST_C0 = 37.75
AT_FIRST0 = 4
AT_CAST_C1 = 5
AT_CAST_W10 = 6.5
AT_LARGER1, AT_FIRST2 = 19.5, 22
AT_CAST_W11 = 5.5
AT_Z_FIRST_LAST = 12


def tile_picked_edgecv_relu_p_kernel(tc, x_words, x_scales, w1, w2, w3_words, w3_scales, offs, cen, pos1, pos2, out):
    nc = tc.nc
    with ExitStack() as ctx:
        keep = ctx.enter_context(tc.tile_pool(name="keep", bufs=1))
        reused = ctx.enter_context(tc.tile_pool(name="reused", bufs=1))
        psum = ctx.enter_context(tc.psum_pool(name="psum", bufs=1))

        def sb(shape, dtype, name, kib=None, tag=None):
            if kib is None:
                return keep.tile(shape, dtype, name=name, tag=tag or name, bufs=1, align_bytes=64)
            return reused.tile(shape, dtype, name=name, align_bytes=64, offset=int(kib * 1024))

        def load_list(src, name):
            tile = keep.tile(list(src.shape), U16, name=name)
            nc.sync.dma_start(tile[:], src)
            return tile

        def load_words(z):
            tile = sb([P, T], I32, "x_table%d" % (z,), AT_WORD_TABLE[z])
            nc.sync.dma_start(tile[:], x_words[z].rearrange("p c r -> p (c r)").bitcast(I32))
            return tile

        def load_weight(w, z, c0, c1, name, kib=None):
            tile = sb([P, PACK, c1 - c0], F32, name, kib)
            nc.sync.dma_start(tile[:], w[z * 512:(z + 1) * 512, c0:c1].rearrange("(p j) c -> p j c", j=PACK))
            return tile

        def scalar_cast(dst, src):
            nc.scalar.activation(dst, src, ACT.Copy)

        def cast_plain(cast, raw, name, kib=None):
            grouped = sb([P, P, PACK], BF16, name + "_grouped", kib)
            cast(grouped[:].rearrange("p (m t) j -> p m j t", t=PACK), raw[:].rearrange("p j (m t) -> p m j t", t=PACK))
            return grouped[:].rearrange("p c j -> p (c j)")

        def cast_paired(raw, name, kib):
            grouped = sb([P, 256, PACK], BF16, name + "_grouped", kib)
            nc.vector.tensor_copy(grouped[:].rearrange("p (u m d) j -> p m j u d", u=2, d=2), raw[:].rearrange("p j (m u d) -> p m j u d", u=2, d=2))
            return grouped[:].rearrange("p c j -> p (c j)")

        def cast_dealt(raw, t0, t1, name, kib):
            grouped = sb([P, t1 - t0, P, PACK], BF16, name + "_grouped", kib)
            nc.vector.tensor_copy(grouped[:].rearrange("p t m j -> p m j t"), raw[:].rearrange("p j (m t) -> p m j t", t=PACK)[:, :, :, t0:t1])
            return grouped[:].rearrange("p t m j -> p (t m j)")

        def quantise(grouped, name, kib=None):
            width = grouped.shape[1] // PACK
            codes = sb([P, width], U32, name + "_codes", kib)
            scales = sb([P, width], U8, name + "_scales")
            nc.vector.quantize_mx(out=codes[:].bitcast(FP8X4), scales=scales[:], in_=grouped)
            return [(codes[:, i:i + P], scales[:, i:i + P]) for i in range(0, width, P)]

        def gather_words(table, name, pieces, tag=None):
            base = pieces[0][0]
            tile = sb([P, pieces[-1][1] - base], U32, name, tag=tag)
            for c0, c1 in pieces:
                nc.vector.tensor_copy(tile[:, c0 - base:c1 - base], table[:].bitcast(U32).indirect(offs_sb[:, c0 // 16:c1 // 16]))
            return tile

        def product(weights, name, pieces=HALVES, order=(0, 1)):
            rows = sb([P, S], F32, name)
            for c0, c1 in pieces:
                acc = psum.tile([P, c1 - c0], F32, name="acc", tag="acc", bufs=BANKS)
                for z in order:
                    for b0, b1, words in picked[z]:
                        u0, u1 = max(b0, c0), min(b1, c1)
                        if u0 < u1:
                            nc.tensor.matmul_mx(
                                out=acc[:, u0 - c0:u1 - c0], lhsT=weights[z][0].bitcast(FP8X4), lhsT_scale=weights[z][1],
                                rhs=words[:, u0 - b0:u1 - b0].bitcast(FP8X4), rhs_scale=picked_scales[4 * z:P, u0:u1],
                                start=(z == order[0] and u0 == c0), stop=(z == order[-1] and u1 == c1))
                nc.scalar.copy(rows[:, c0:c1], acc[:])
            return rows

        x_scale_table = sb([P, SCALE_TABLE_KIB * 1024], U8, "x_scale_table", 0)
        nc.vector.memset(x_scale_table[32:64, 0:T].bitcast(I32), 0)
        nc.vector.memset(x_scale_table[64:P, 0:T].bitcast(I32), 0)
        for z in range(PASSES):
            (nc.scalar, nc.sync)[z].dma_start(x_scale_table[z:32:2, 0:T].bitcast(I32), x_scales[z].bitcast(I32))
        offs_sb = load_list(offs, "offs_sb")
        table0 = load_words(0)
        pos1_sb = load_list(pos1, "pos1_sb")
        pos2_sb = load_list(pos2, "pos2_sb")
        cen_sb = load_list(cen, "cen_sb")
        table1 = load_words(1)
        raw_a = [load_weight(w2, z, 0, 128, "raw_a%d" % z) for z in range(PASSES)]

        scale_rows = sb([P, S], U8, "scale_rows")
        nc.vector.tensor_copy(scale_rows[:], x_scale_table[:, 0:T].indirect(offs_sb[:]))
        picked_scales = sb([P, S], U8, "picked_scales")
        for r in range(4):
            nc.sync.dma_start(picked_scales[r:P:4, :].bitcast(I32), scale_rows[2 * r:2 * r + 32, :].bitcast(I32))

        raw_b = [load_weight(w2, z, 128, 256, "raw_b%d" % z, AT_RAW_B[z]) for z in range(PASSES)]
        raw_c = [load_weight(w2, z, 256, H, "raw_c%d" % z, AT_RAW_C[z]) for z in range(PASSES)]
        raw_w1 = [load_weight(w1, z, 0, H, "raw_w1%d" % z, AT_RAW_W1[z]) for z in range(PASSES)]
        w3_code = sb([P, N], U32, "w3_code", AT_W3_WORDS)
        nc.sync.dma_start(w3_code[:].bitcast(I32), w3_words[0].rearrange("p c r -> p (c r)").bitcast(I32))
        w3_scale = sb([P, N], U8, "w3_scale", AT_W3_SCALES)
        nc.vector.memset(w3_scale[:].bitcast(I32), 0)
        for q in range(4):
            nc.sync.dma_start(w3_scale[32 * q:32 * q + 4, :].bitcast(I32), w3_scales[0, 4 * q:4 * q + 4, :].bitcast(I32))

        picked0 = gather_words(table0, "x_picked0", HALVES)
        picked1 = gather_words(table1, "x_picked1", TAPERED[0:1])
        qa = quantise(cast_plain(scalar_cast, raw_a[0], "wa0"), "wa0")
        picked2 = gather_words(table1, "x_picked2", TAPERED[1:2], tag="raw_a0")
        qa = qa + quantise(cast_plain(scalar_cast, raw_a[1], "wa1"), "wa1")
        picked3 = gather_words(table1, "x_picked3", TAPERED[2:3], tag="raw_a1")
        picked = [[(0, S, picked0)], [(0, 512, picked1), (512, 768, picked2), (768, S, picked3)]]
        qb = quantise(cast_plain(scalar_cast, raw_b[0], "wb0"), "wb0", AT_CODES_B0)

        edge = sb([P, PACK, V], F32, "edge")
        dealt = [sb([P, V], F32, "larger%d" % (t,)) for t in range(PACK)]

        def vector_fetch(rows, places, name, kib=None):
            tile = sb([P, V], F32, name, kib)
            nc.vector.tensor_copy(tile[:], rows[:].indirect(places[:]))
            return tile

        def scalar_fetch(rows, places, name):
            tile = sb([P, V], F32, name)
            nc.scalar.activation(tile[:], rows[:].indirect(places[:]), ACT.Copy)
            return tile

        def larger(first, second, c0, width, t0, kib=None):
            tile = sb([P, V], F32, "unplaced%d_%d" % (c0, t0), kib)
            run = width // PACK
            rows = slice(c0 // PACK, c0 // PACK + run)
            nc.vector.tensor_tensor(tile[:], first[:], second[:], ALU.max)
            for u in range(P // run):
                nc.sync.dma_start(dealt[t0 + u][rows, :], tile[u:P:P // run, :])

        def add_centres(v0, v1, t):
            nc.vector.tensor_tensor(edge[:, t, v0:v1], y[t][:].indirect(cen_sb[:, v0 // 16:v1 // 16]), dealt[t][:, v0:v1], ALU.add)

        cast_b1 = cast_plain(nc.vector.tensor_copy, raw_b[1], "wb1", AT_CAST_B1)
        e0 = product(qa, "e0", TAPERED)
        qb = qb + quantise(cast_b1, "wb1", AT_CODES_B1)
        first0 = vector_fetch(e0, pos1_sb, "first0", AT_FIRST0)
        second0 = scalar_fetch(e0, pos2_sb, "second0")
        cast_c0 = cast_paired(raw_c[0], "wc0", AT_CAST_C0)
        larger(first0, second0, 0, 128, 0)
        qc = quantise(cast_c0, "wc0")
        qc = qc + quantise(cast_paired(raw_c[1], "wc1", AT_CAST_C1), "wc1")
        e1 = product(qb, "e1")
        second1 = scalar_fetch(e1, pos2_sb, "second1")
        first1 = scalar_fetch(e1, pos1_sb, "first1")
        cast_w10 = cast_dealt(raw_w1[0], 0, 4, "w10", AT_CAST_W10)
        larger(first1, second1, 128, 128, 0, AT_LARGER1)
        q10 = quantise(cast_w10, "w10")
        e2 = product([qc[0], qc[2]], "e2")
        second2 = scalar_fetch(e2, pos2_sb, "second2")
        first2 = vector_fetch(e2, pos1_sb, "first2", AT_FIRST2)
        cast_w11 = cast_dealt(raw_w1[1], 0, 2, "w11a", AT_CAST_W11)
        larger(first2, second2, 256, 256, 0)
        q11 = quantise(cast_w11, "w11a")
        e3 = product([qc[1], qc[3]], "e3", order=(1, 0))
        second3 = scalar_fetch(e3, pos2_sb, "second3")
        first3 = vector_fetch(e3, pos1_sb, "first3")
        cast_w11 = cast_dealt(raw_w1[1], 2, 4, "w11b", AT_CAST_W11)
        larger(first3, second3, 256, 256, 2)
        q11 = q11 + quantise(cast_w11, "w11b")
        y = [product([q10[t], q11[t]], "y%d" % (t,)) for t in range(PACK)]

        def relu_views(z_tile, base, v0, v1):
            return (z_tile[:, v0 - base:v1 - base].rearrange("p (c i) t -> p c t i", i=4), edge[:, :, v0:v1].rearrange("p t (c i) -> p c t i", i=4))

        def project(name, z_tiles, copy, res_sb):
            n = sum(z_tile.shape[1] for z_tile in z_tiles)
            z_codes = sb([P, n], U32, name + "_codes")
            z_scales = sb([P, n], U8, name + "_scales")
            c0 = 0
            for z_tile in z_tiles:
                c1 = c0 + z_tile.shape[1]
                nc.vector.quantize_mx(out=z_codes[:, c0:c1].bitcast(FP8X4), scales=z_scales[:, c0:c1], in_=z_tile[:].rearrange("p c t -> p (c t)"))
                c0 = c1
            res = psum.tile([P, n], F32, name="res", tag="acc", bufs=BANKS)
            nc.tensor.matmul_mx(out=res[:], lhsT=w3_code[:].bitcast(FP8X4), lhsT_scale=w3_scale[:],
                                rhs=z_codes[:].bitcast(FP8X4), rhs_scale=z_scales[:], start=True, stop=True)
            copy(res_sb, res[:])

        for t in (0, 1):
            add_centres(0, V, t)
        for v0, v1, pieces in ((0, 256, 2), (256, 384, 1), (384, 512, 2)):
            add_centres(v0, v1, 2)
            step = (v1 - v0) // pieces
            for u0 in range(v0, v1, step):
                add_centres(u0, u0 + step, 3)
        za = sb([P, 256, PACK], BF16, "za", AT_Z_FIRST_LAST)
        zb = sb([P, 128, PACK], BF16, "zb")
        zc = sb([P, 64, PACK], BF16, "zc")
        for z_tile, base, v0, v1 in ((za, 0, 0, 128), (za, 0, 128, 256), (zb, 256, 256, 384), (zc, 384, 384, 448)):
            dst, src = relu_views(z_tile, base, v0, v1)
            nc.scalar.activation(dst, src, ACT.Relu)
        res_a = sb([P, 256], F32, "res_a")
        res_b = sb([P, 256], F32, "res_b")
        project("za", [za], nc.scalar.copy, res_a[:])
        nc.sync.dma_start(out[:, 0:256], res_a[:])
        zd = sb([P, 64, PACK], BF16, "zd", AT_Z_FIRST_LAST)
        dst, src = relu_views(zd, 448, 448, 512)
        nc.vector.tensor_scalar_max(dst, src, 0.0)
        project("zb", [zb], nc.scalar.copy, res_b[:, 0:128])
        project("zc", [zc, zd], nc.vector.tensor_copy, res_b[:, 128:256])
        nc.sync.dma_start(out[:, 256:V], res_b[:])
